import numpy as np
import ml_dtypes


def mxq(x, axis, fmt="e4m3"):
    dtype, down = {"e4m3": (ml_dtypes.float8_e4m3fn, 7), "e5m2": (ml_dtypes.float8_e5m2, 14)}[fmt]
    v = np.moveaxis(np.asarray(x, np.float32).astype(ml_dtypes.bfloat16).astype(np.float64), axis, -1)
    blocks = v.reshape(v.shape[:-1] + (-1, 32))
    amax = np.abs(blocks).max(-1, keepdims=True)
    byte = np.maximum(np.where(amax > 0, np.frexp(amax)[1] - 1 + 127, 0) - down, 1)
    scale = np.exp2(byte - 127.0)
    codes = (blocks / scale).astype(np.float32).astype(dtype).astype(np.float64)
    return np.moveaxis((codes * scale).reshape(v.shape), -1, axis)


WIDE = False


def mx_kscale(k):
    if not WIDE:
        return np.ones(k)
    levels = np.array([10, -10, 5, -5, 0])
    if k % 512:
        return np.exp2(np.random.permutation(np.resize(levels, k // 32))).repeat(32)
    a = np.empty((k // 512, 16))
    for p in range(k // 512):
        a[p, :8] = np.random.permutation(np.resize(levels, 8))
        for g in range(8):
            far = levels[np.abs(levels - a[p, g]) >= 10]
            a[p, g + 8] = far[np.random.randint(len(far))]
    return np.exp2(a.ravel()).repeat(32)


def f64(x):
    return np.asarray(x).astype(np.float64)


def striped(idx):
    return np.tile(idx.reshape(-1, 16).T, (8, 1)).astype(np.uint16)


def unstriped(offs):
    return offs[:16].T.reshape(-1).astype(np.int64)


E2M1 = np.array([0.0, 0.5, 1.0, 1.5, 2.0, 3.0, 4.0, 6.0, -0.0, -0.5, -1.0, -1.5, -2.0, -3.0, -4.0, -6.0])


def pack_weight(w, fmt):
    k, n = w.shape
    w = f64(np.asarray(w, np.float32).astype(ml_dtypes.bfloat16)).reshape(k // 32, 32, n)
    amax = np.abs(w).max(1)
    if fmt == "e4m3":
        byte = np.frexp(amax)[1] - 1 + 127 - 7
    else:
        mant, ex = np.frexp(amax / 6.0)
        byte = np.where(mant > 0.5, ex, ex - 1) + 127
    byte = np.clip(np.where(amax > 0, byte, 1), 1, 254)
    scaled = (w * np.exp2(127.0 - byte)[:, None, :]).reshape(k, n).astype(np.float32)
    by_word = np.ascontiguousarray(scaled.reshape(k // 512, 128, 4, n).transpose(0, 1, 3, 2))
    if fmt == "e4m3":
        words = by_word.astype(ml_dtypes.float8_e4m3fn).view(np.uint8)
    else:
        c = by_word.astype(ml_dtypes.float4_e2m1fn).view(np.uint8) & 0xF
        words = (c[..., 0::2] | (c[..., 1::2] << 4)).reshape(k // 512, 128, 2 * n)
    return np.ascontiguousarray(words), np.ascontiguousarray(byte.astype(np.uint8).reshape(k // 512, 16, n))


def unpack_weight(words, scales, fmt):
    g, _, n = scales.shape
    words = np.ascontiguousarray(words).reshape(g, 128, n, -1)
    if fmt == "e4m3":
        vals = words.view(ml_dtypes.float8_e4m3fn).astype(np.float64)
    else:
        nib = np.empty((g, 128, n, 4), np.uint8)
        nib[..., 0::2] = words & 0xF
        nib[..., 1::2] = words >> 4
        vals = E2M1[nib]
    vals = vals * np.repeat(np.exp2(scales.astype(np.float64) - 127.0), 8, axis=1)[..., None]
    return vals.transpose(0, 1, 3, 2).reshape(g * 512, n)


def gelu(v):
    return 0.5 * v * (1.0 + np.tanh(np.sqrt(2.0 / np.pi) * (v + 0.044715 * v**3)))


K, T, E, C, H, N = 1024, 512, 8, 128, 512, 128


def by_expert(wq, xq):
    return np.concatenate([wq[e].T @ xq[:, e * C:(e + 1) * C] for e in range(E)], axis=1)


def setup_inputs():
    n = np.random.standard_normal
    s = mx_kscale(K)
    u = mx_kscale(H)
    first = np.random.permutation(np.repeat(np.arange(E), T // E))
    second = (first + 1 + np.random.permutation(np.repeat(np.arange(E - 1), -(-T // (E - 1)))[:T])) % E
    while np.bincount(second, minlength=E).max() != T // E:
        load = np.bincount(second, minlength=E); hi, lo = int(load.argmax()), int(load.argmin())
        t = np.flatnonzero((second == hi) & (first != lo))[0]; second[t] = lo
    slot_token = np.empty(E * C, np.int64); pos = np.empty((2, T), np.int64); fill = np.zeros(E, np.int64)
    place = np.stack([np.random.permutation(C) for _ in range(E)])
    for r, deal in enumerate((first, second)):
        for t in np.random.permutation(T):
            e = deal[t]; j = e * C + place[e, fill[e]]; fill[e] += 1; slot_token[j] = t; pos[r, t] = j
    g = np.random.uniform(0.2, 0.8, T)
    x = pack_weight(n((K, T)) * s[:, None], "e4m3")
    w = [pack_weight(m, "e2m1") for m in n((E, K, N)) / np.sqrt(K) / s[None, :, None]]
    wa = [pack_weight(m, "e4m3") for m in n((E, K, H)) / np.sqrt(K) / s[None, :, None] * u]
    wb = [pack_weight(m, "e4m3") for m in n((E, H, N)) / np.sqrt(H) / u[None, :, None]]
    return {
        "x_words": x[0],
        "x_scales": x[1],
        "w_words": np.stack([m[0] for m in w]),
        "w_scales": np.stack([m[1] for m in w]),
        "wa_words": np.stack([m[0] for m in wa]),
        "wa_scales": np.stack([m[1] for m in wa]),
        "wb_words": np.stack([m[0] for m in wb]),
        "wb_scales": np.stack([m[1] for m in wb]),
        "gate": np.stack([np.tile(g, (128, 1)), np.tile(1.0 - g, (128, 1))]).astype(np.float32),
        "offs": striped(slot_token),
        "pos1": striped(pos[0]),
        "pos2": striped(pos[1]),
    }


def reference(x_words, x_scales, w_words, w_scales, wa_words, wa_scales, wb_words, wb_scales, gate, offs, pos1, pos2):
    w = np.stack([unpack_weight(w_words[e], w_scales[e], "e2m1") for e in range(E)])
    wa = np.stack([unpack_weight(wa_words[e], wa_scales[e], "e4m3") for e in range(E)])
    wb = np.stack([unpack_weight(wb_words[e], wb_scales[e], "e4m3") for e in range(E)])
    idx = unstriped(offs)
    xq = unpack_weight(x_words, x_scales, "e4m3")[:, idx]
    h = gelu(by_expert(wa, xq))
    y = by_expert(w, xq) + by_expert(wb, mxq(h, 0, "e4m3"))
    out = sum(f64(gate[r, :1]) * y[:, unstriped(p)] for r, p in enumerate((pos1, pos2)))
    return out

@@ -1,0 +1,295 @@
+from contextlib import ExitStack
+
+import concourse.mybir as mybir
+from concourse.masks import make_identity
+
+K, T, E, C, H, N = 1024, 512, 8, 128, 512, 128
+S = E * C
+P = 128
+PASSES = 2
+
+F32 = mybir.dt.float32
+BF16 = mybir.dt.bfloat16
+I32 = mybir.dt.int32
+U32 = mybir.dt.uint32
+U16 = mybir.dt.uint16
+U8 = mybir.dt.uint8
+FP8X4 = mybir.dt.float8_e4m3fn_x4
+FP4X4 = mybir.dt.float4_e2m1fn_x4
+GELU = mybir.ActivationFunctionType.Gelu_apprx_tanh
+MULT = mybir.AluOpType.mult
+ADD = mybir.AluOpType.add
+
+FLOPS = 2 * S * (K * H + K * N + H * N)
+
+WA_ROW = (12, 4)
+WB_ROW = 8
+
+
+def tile_moe_elr_gelu_kernel(
+    tc, x_words, x_scales, w_words, w_scales, wa_words, wa_scales, wb_words, wb_scales, gate, offs, pos1, pos2, out
+):
+    nc = tc.nc
+    with ExitStack() as ctx:
+        keep = ctx.enter_context(tc.tile_pool(name="keep", bufs=1))
+        ring = ctx.enter_context(tc.tile_pool(name="ring", bufs=3))
+        psum_h = ctx.enter_context(tc.psum_pool(name="psum_h", bufs=3))
+        psum_y = ctx.enter_context(tc.psum_pool(name="psum_y", bufs=2))
+
+        offs_sb = keep.tile([P, S // 16], U16, name="offs_sb")
+        pos_sb = [keep.tile([P, T // 16], U16, name="pos%d_sb" % r) for r in range(2)]
+        x_tok = [keep.tile([P, T], I32, name="x_tok%d" % s, align_bytes=64) for s in range(PASSES)]
+        xs_tok = keep.tile([P, PASSES, T], U8, name="xs_tok", align_bytes=64)
+        x_slot = [keep.tile([P, S], I32, name="x_slot%d" % s, align_bytes=64) for s in range(PASSES)]
+        xs_slot = [keep.tile([P, S], U8, name="xs_slot%d" % s, align_bytes=64) for s in range(PASSES)]
+        wa_sb = keep.tile([P, E * PASSES, H], I32, name="wa_sb", align_bytes=64)
+        was_sb = [keep.tile([P, E // 2 * PASSES, H], U8, name="was_sb%d" % g, align_bytes=64) for g in range(2)]
+        w_sb = keep.tile([P, E * PASSES, 2 * N], U8, name="w_sb", align_bytes=64)
+        ws_sb = keep.tile([P, E * PASSES, N], U8, name="ws_sb", align_bytes=64)
+        wb_sb = keep.tile([P, E, N], I32, name="wb_sb", align_bytes=64)
+        wbs_sb = keep.tile([P, E, N], U8, name="wbs_sb", align_bytes=64)
+        gate_sb = [keep.tile([P, T], F32, name="gate%d_sb" % r) for r in range(2)]
+        ident = keep.tile([P, P], F32, name="ident")
+        y_sb = keep.tile([P, S], F32, name="y_sb")
+        warm = keep.tile([P, 2], F32, name="warm")
+        gate_rows = keep.tile([P, P], F32, name="gate_rows")
+        gate_cols = keep.tile([P, 8], F32, name="gate_cols")
+
+        def load_wa(e0, e1):
+            nc.sync.dma_start(
+                wa_sb[:, PASSES * e0 : PASSES * e1, :],
+                wa_words[e0:e1].rearrange("e s p i d -> p (e s) (i d)").bitcast(I32),
+            )
+
+        def load_w(e0, e1):
+            nc.sync.dma_start(
+                w_sb[:, PASSES * e0 : PASSES * e1, :].bitcast(I32),
+                w_words[e0:e1].rearrange("e s p b -> p (e s) b").bitcast(I32),
+            )
+
+        def load_wb(e0, e1):
+            nc.sync.dma_start(
+                wb_sb[:, e0:e1, :], wb_words[e0:e1].rearrange("e o p n d -> p (e o) (n d)").bitcast(I32)
+            )
+
+        def load_was(queue, g, q):
+            row = 32 * q + WA_ROW[g]
+            queue.dma_start(
+                was_sb[g][row : row + 4, :, :].bitcast(I32),
+                wa_scales[4 * g : 4 * g + 4, :, 4 * q : 4 * q + 4, :].rearrange("e s r i -> r (e s) i").bitcast(I32),
+            )
+
+        def load_ws(q):
+            nc.gpsimd.dma_start(
+                ws_sb[32 * q : 32 * q + 4, :, :].bitcast(I32),
+                w_scales[:, :, 4 * q : 4 * q + 4, :].rearrange("e s r n -> r (e s) n").bitcast(I32),
+            )
+
+        def load_wbs(q):
+            row = 32 * q + WB_ROW
+            nc.sync.dma_start(
+                wbs_sb[row : row + 4, :, :].bitcast(I32),
+                wb_scales[:, 0, 4 * q : 4 * q + 4, :].rearrange("e r n -> r e n").bitcast(I32),
+            )
+
+        def gather_bytes(j0, j1):
+            for s in range(PASSES):
+                nc.vector.tensor_copy(
+                    xs_slot[s][:, j0:j1], xs_tok[:, s, :].indirect(offs_sb[:, j0 // 16 : j1 // 16])
+                )
+
+        def gather_words(j0, j1):
+            for s in range(PASSES):
+                nc.vector.tensor_copy(
+                    x_slot[s][:, j0:j1].bitcast(U32),
+                    x_tok[s][:].bitcast(U32).indirect(offs_sb[:, j0 // 16 : j1 // 16]),
+                )
+
+        nc.vector.memset(xs_tok[:].rearrange("p s t -> p (s t)").bitcast(I32), 0)
+        nc.vector.memset(warm[:, 0:1], 0.0)
+        nc.scalar.activation(warm[:, 1:2], warm[:, 0:1], GELU)
+
+        nc.vector.memset(gate_rows[:], 0.0)
+        make_identity(nc, ident[:])
+        nc.gpsimd.dma_start(gate_rows[0:8, :], gate[:, 0, :].rearrange("r (c j) -> r c j", j=P))
+        for q in range(4):
+            load_ws(q)
+
+        nc.sync.dma_start(offs_sb[:], offs)
+        nc.sync.dma_start(x_tok[0][:], x_words[0].rearrange("p t d -> p (t d)").bitcast(I32))
+        for q in range(4):
+            nc.sync.dma_start(
+                xs_tok[32 * q : 32 * q + 4, :, :].bitcast(I32),
+                x_scales[:, 4 * q : 4 * q + 4, :].rearrange("s r t -> r s t").bitcast(I32),
+            )
+        nc.sync.dma_start(x_tok[1][:], x_words[1].rearrange("p t d -> p (t d)").bitcast(I32))
+        load_wa(0, 2)
+        for q in range(4):
+            load_was(nc.sync, 0, q)
+        load_wa(2, 4)
+        for q in range(4):
+            load_was(nc.sync, 1, q)
+        load_wa(4, 6)
+        for q in range(4):
+            load_wbs(q)
+        load_w(0, 4)
+        load_wa(6, 7)
+        nc.sync.dma_start(pos_sb[0][:], pos1)
+        nc.sync.dma_start(pos_sb[1][:], pos2)
+        for a in range(2):
+            nc.sync.dma_start(
+                wa_sb[:, PASSES * (E - 1) :, a * (H // 2) : (a + 1) * (H // 2)],
+                wa_words[E - 1, :, :, a * (H // 2) : (a + 1) * (H // 2), :]
+                .rearrange("s p i d -> p s (i d)")
+                .bitcast(I32),
+            )
+        load_wb(0, 4)
+        load_w(4, E)
+        load_wb(4, E)
+
+        gate_turned = psum_y.tile([P, T], F32, name="y")
+        nc.tensor.transpose(gate_turned[:, 0:P], gate_rows[:], ident[:])
+        nc.scalar.copy(gate_cols[:], gate_turned[:, 0:8])
+        for r in range(2):
+            spread = psum_h.tile([P, H], F32, name="bank%d" % r)
+            for c in range(4):
+                a = 4 * r + c
+                nc.tensor.transpose(
+                    spread[:, c * P : (c + 1) * P], gate_cols[:, a : a + 1].to_broadcast([P, P]), ident[:]
+                )
+            nc.scalar.copy(gate_sb[r][:], spread[:])
+
+        gather_bytes(0, 256)
+        gather_words(0, 128)
+        gather_words(128, 256)
+        for j in range(256, S, 256):
+            gather_bytes(j, j + 256)
+            gather_words(j, j + 256)
+
+        h_words = {}
+        banks = {}
+        half_h = H // 2
+
+        def first_layer(e):
+            cols = slice(e * C, (e + 1) * C)
+            banks[e] = [psum_h.tile([P, H], F32, name="bank%d" % a) for a in range(2)]
+            for a in range(2):
+                hid = slice(a * half_h, (a + 1) * half_h)
+                for s in range(PASSES):
+                    nc.tensor.matmul_mx(
+                        banks[e][a][:, 0:half_h],
+                        lhsT=x_slot[s][:, cols].bitcast(FP8X4),
+                        lhsT_scale=xs_slot[s][:, cols],
+                        rhs=wa_sb[:, PASSES * e + s, hid].bitcast(FP8X4),
+                        rhs_scale=was_sb[e // 4][WA_ROW[e // 4] : P, PASSES * (e % 4) + s, hid],
+                        start=(s == 0),
+                        stop=(s == PASSES - 1),
+                    )
+
+        def activate(e, a):
+            if a == 0:
+                h_words[e] = ring.tile([P, H], BF16, name="h", align_bytes=64)
+            nc.scalar.activation(
+                h_words[e][:].rearrange("j (u p b) -> j u p b", u=2, b=2)[:, :, 64 * a : 64 * (a + 1), :],
+                banks[e][a][:, 0:half_h].rearrange("j (p u b) -> j u p b", u=2, b=2),
+                GELU,
+            )
+
+        turned = {}
+
+        def turn(e):
+            words = h_words[e][:].bitcast(F32)
+            if e + 1 < E:
+                bank = banks[e + 1][1]
+            else:
+                bank = psum_h.tile([P, H], F32, name="bank1")
+            turned[e] = bank[:, half_h:H].rearrange("p (u j) -> p u j", u=2)
+            for u in range(2):
+                nc.tensor.transpose(turned[e][:, u, :], words[:, u * P : (u + 1) * P], ident[:])
+
+        grouped = keep.tile([P, E, 4 * C], BF16, name="grouped", align_bytes=64)
+        h_codes = keep.tile([P, S], U32, name="h_codes", align_bytes=64)
+        h_scales = keep.tile([P, S], U8, name="h_scales", align_bytes=64)
+
+        def regroup(e):
+            nc.scalar.copy(
+                grouped[:, e, :].bitcast(F32).rearrange("p (j u) -> p j u", u=2),
+                turned[e].rearrange("p u j -> p j u"),
+            )
+
+        def quantise(e0, e1):
+            cols = slice(e0 * C, e1 * C)
+            nc.vector.quantize_mx(
+                h_codes[:, cols].bitcast(FP8X4),
+                h_scales[:, cols],
+                grouped[:, e0:e1, :].rearrange("p e f -> p (e f)"),
+            )
+
+        def second_layer(e0, e1, evacuate):
+            y = psum_y.tile([P, T], F32, name="y")
+            for e in range(e0, e1):
+                cols = slice(e * C, (e + 1) * C)
+                acc = y[:, (e - e0) * C : (e - e0 + 1) * C]
+                for s in range(PASSES):
+                    nc.tensor.matmul_mx(
+                        acc,
+                        lhsT=w_sb[:, PASSES * e + s, :].bitcast(FP4X4),
+                        lhsT_scale=ws_sb[:, PASSES * e + s, :],
+                        rhs=x_slot[s][:, cols].bitcast(FP8X4),
+                        rhs_scale=xs_slot[s][:, cols],
+                        start=(s == 0),
+                        stop=False,
+                    )
+                nc.tensor.matmul_mx(
+                    acc,
+                    lhsT=wb_sb[:, e, :].bitcast(FP8X4),
+                    lhsT_scale=wbs_sb[WB_ROW:P, e, :],
+                    rhs=h_codes[:, cols].bitcast(FP8X4),
+                    rhs_scale=h_scales[:, cols],
+                    start=False,
+                    stop=True,
+                )
+            evacuate(y_sb[:, e0 * C : e1 * C], y[:, 0 : (e1 - e0) * C])
+
+        for step in range(E + 1):
+            if step < E:
+                first_layer(step)
+                activate(step, 0)
+            if step >= 1:
+                turn(step - 1)
+            if step < E:
+                activate(step, 1)
+            if step >= 1:
+                regroup(step - 1)
+            if step in (2, 4, 6):
+                quantise(step - 2, step)
+            if step >= 7:
+                quantise(step - 1, step)
+        second_layer(0, 4, nc.vector.tensor_copy)
+        second_layer(4, 7, nc.vector.tensor_copy)
+        second_layer(7, 8, nc.scalar.copy)
+
+        half = T // 2
+        prod = [keep.tile([P, T], F32, name="prod%d" % r) for r in range(2)]
+        res = [keep.tile([P, half], F32, name="res%d" % a) for a in range(2)]
+
+        def combine(r, a):
+            cols = slice(a * half, (a + 1) * half)
+            nc.vector.tensor_tensor(
+                prod[r][:, cols],
+                y_sb[:].indirect(pos_sb[r][:, a * half // 16 : (a + 1) * half // 16]),
+                gate_sb[r][:, cols],
+                MULT,
+            )
+
+        def finish(a):
+            cols = slice(a * half, (a + 1) * half)
+            nc.vector.tensor_tensor(res[a][:], prod[0][:, cols], prod[1][:, cols], ADD)
+            nc.sync.dma_start(out[:, cols], res[a][:])
+
+        combine(0, 0)
+        combine(1, 0)
+        combine(0, 1)
+        finish(0)
+        combine(1, 1)
+        finish(1)

@@ -22,6 +22,7 @@ ADD = mybir.AluOpType.add
 
 FLOPS = 2 * S * (K * H + K * N + H * N)
 
+X_ROW = (0, 4)
 WA_ROW = (12, 4)
 WB_ROW = 8
 
@@ -32,14 +33,14 @@ def tile_moe_elr_gelu_kernel(
     nc = tc.nc
     with ExitStack() as ctx:
         keep = ctx.enter_context(tc.tile_pool(name="keep", bufs=1))
-        ring = ctx.enter_context(tc.tile_pool(name="ring", bufs=3))
+        ring = ctx.enter_context(tc.tile_pool(name="ring", bufs=4))
         psum_h = ctx.enter_context(tc.psum_pool(name="psum_h", bufs=3))
         psum_y = ctx.enter_context(tc.psum_pool(name="psum_y", bufs=2))
 
         offs_sb = keep.tile([P, S // 16], U16, name="offs_sb")
         pos_sb = [keep.tile([P, T // 16], U16, name="pos%d_sb" % r) for r in range(2)]
-        x_tok = [keep.tile([P, T], I32, name="x_tok%d" % s, align_bytes=64) for s in range(PASSES)]
-        xs_tok = keep.tile([P, PASSES, T], U8, name="xs_tok", align_bytes=64)
+        x_tok = keep.tile([P, PASSES, T], I32, name="x_tok", align_bytes=64)
+        xs_tok = keep.tile([P, T], U8, name="xs_tok", align_bytes=64)
         x_slot = [keep.tile([P, S], I32, name="x_slot%d" % s, align_bytes=64) for s in range(PASSES)]
         xs_slot = [keep.tile([P, S], U8, name="xs_slot%d" % s, align_bytes=64) for s in range(PASSES)]
         wa_sb = keep.tile([P, E * PASSES, H], I32, name="wa_sb", align_bytes=64)
@@ -52,11 +53,9 @@ def tile_moe_elr_gelu_kernel(
         ident = keep.tile([P, P], F32, name="ident")
         y_sb = keep.tile([P, S], F32, name="y_sb")
         warm = keep.tile([P, 2], F32, name="warm")
-        gate_rows = keep.tile([P, P], F32, name="gate_rows")
-        gate_cols = keep.tile([P, 8], F32, name="gate_cols")
 
-        def load_wa(e0, e1):
-            nc.sync.dma_start(
+        def load_wa(queue, e0, e1):
+            queue.dma_start(
                 wa_sb[:, PASSES * e0 : PASSES * e1, :],
                 wa_words[e0:e1].rearrange("e s p i d -> p (e s) (i d)").bitcast(I32),
             )
@@ -79,63 +78,80 @@ def tile_moe_elr_gelu_kernel(
                 wa_scales[4 * g : 4 * g + 4, :, 4 * q : 4 * q + 4, :].rearrange("e s r i -> r (e s) i").bitcast(I32),
             )
 
-        def load_ws(q):
-            nc.gpsimd.dma_start(
+        def load_ws(queue, q):
+            queue.dma_start(
                 ws_sb[32 * q : 32 * q + 4, :, :].bitcast(I32),
                 w_scales[:, :, 4 * q : 4 * q + 4, :].rearrange("e s r n -> r (e s) n").bitcast(I32),
             )
 
-        def load_wbs(q):
+        def load_wbs(queue, q):
             row = 32 * q + WB_ROW
-            nc.sync.dma_start(
+            queue.dma_start(
                 wbs_sb[row : row + 4, :, :].bitcast(I32),
                 wb_scales[:, 0, 4 * q : 4 * q + 4, :].rearrange("e r n -> r e n").bitcast(I32),
             )
 
         def gather_bytes(j0, j1):
-            for s in range(PASSES):
-                nc.vector.tensor_copy(
-                    xs_slot[s][:, j0:j1], xs_tok[:, s, :].indirect(offs_sb[:, j0 // 16 : j1 // 16])
-                )
+            nc.vector.tensor_copy(xs_slot[0][:, j0:j1], xs_tok[:].indirect(offs_sb[:, j0 // 16 : j1 // 16]))
 
         def gather_words(j0, j1):
             for s in range(PASSES):
                 nc.vector.tensor_copy(
                     x_slot[s][:, j0:j1].bitcast(U32),
-                    x_tok[s][:].bitcast(U32).indirect(offs_sb[:, j0 // 16 : j1 // 16]),
+                    x_tok[:, s, :].bitcast(U32).indirect(offs_sb[:, j0 // 16 : j1 // 16]),
                 )
 
-        nc.vector.memset(xs_tok[:].rearrange("p s t -> p (s t)").bitcast(I32), 0)
+        nc.vector.memset(xs_tok[:].bitcast(I32), 0)
         nc.vector.memset(warm[:, 0:1], 0.0)
         nc.scalar.activation(warm[:, 1:2], warm[:, 0:1], GELU)
 
-        nc.vector.memset(gate_rows[:], 0.0)
         make_identity(nc, ident[:])
-        nc.gpsimd.dma_start(gate_rows[0:8, :], gate[:, 0, :].rearrange("r (c j) -> r c j", j=P))
         for q in range(4):
-            load_ws(q)
+            load_ws(nc.gpsimd, q)
+        for q in range(2):
+            load_wbs(nc.gpsimd, q)
+
+        def move_scales(q):
+            nc.sync.dma_start(
+                xs_slot[1][32 * q : 32 * q + 4, :].bitcast(I32),
+                xs_slot[0][32 * q + 4 : 32 * q + 8, :].bitcast(I32),
+            )
 
         nc.sync.dma_start(offs_sb[:], offs)
-        nc.sync.dma_start(x_tok[0][:], x_words[0].rearrange("p t d -> p (t d)").bitcast(I32))
         for q in range(4):
             nc.sync.dma_start(
-                xs_tok[32 * q : 32 * q + 4, :, :].bitcast(I32),
-                x_scales[:, 4 * q : 4 * q + 4, :].rearrange("s r t -> r s t").bitcast(I32),
+                xs_tok[32 * q : 32 * q + 8, :].bitcast(I32), x_scales[:, 4 * q : 4 * q + 4, :].bitcast(I32)
             )
-        nc.sync.dma_start(x_tok[1][:], x_words[1].rearrange("p t d -> p (t d)").bitcast(I32))
-        load_wa(0, 2)
-        for q in range(4):
+        nc.sync.dma_start(x_tok[:], x_words.rearrange("s p t d -> p s (t d)").bitcast(I32))
+        load_was(nc.sync, 0, 0)
+        load_wa(nc.sync, 0, 1)
+        for q in range(1, 4):
             load_was(nc.sync, 0, q)
-        load_wa(2, 4)
+        load_wa(nc.sync, 1, 2)
+        load_wa(nc.sync, 2, 3)
         for q in range(4):
             load_was(nc.sync, 1, q)
-        load_wa(4, 6)
-        for q in range(4):
-            load_wbs(q)
+        load_wa(nc.sync, 3, 4)
         load_w(0, 4)
-        load_wa(6, 7)
-        nc.sync.dma_start(pos_sb[0][:], pos1)
-        nc.sync.dma_start(pos_sb[1][:], pos2)
+
+        gather_bytes(0, 256)
+        gather_words(0, 128)
+        gather_words(128, 256)
+        gather_bytes(256, 640)
+        gather_bytes(640, 1024)
+        for j in range(256, S, 256):
+            gather_words(j, j + 256)
+
+        move_scales(0)
+        move_scales(1)
+        load_wa(nc.sync, 4, 5)
+        move_scales(2)
+        move_scales(3)
+        load_wa(nc.sync, 5, 6)
+        load_wbs(nc.sync, 2)
+        load_wbs(nc.sync, 3)
+        load_wa(nc.sync, 6, 7)
+        load_wb(0, 4)
         for a in range(2):
             nc.sync.dma_start(
                 wa_sb[:, PASSES * (E - 1) :, a * (H // 2) : (a + 1) * (H // 2)],
@@ -143,28 +159,12 @@ def tile_moe_elr_gelu_kernel(
                 .rearrange("s p i d -> p s (i d)")
                 .bitcast(I32),
             )
-        load_wb(0, 4)
         load_w(4, E)
         load_wb(4, E)
-
-        gate_turned = psum_y.tile([P, T], F32, name="y")
-        nc.tensor.transpose(gate_turned[:, 0:P], gate_rows[:], ident[:])
-        nc.scalar.copy(gate_cols[:], gate_turned[:, 0:8])
+        nc.sync.dma_start(pos_sb[0][:], pos1)
+        nc.sync.dma_start(pos_sb[1][:], pos2)
         for r in range(2):
-            spread = psum_h.tile([P, H], F32, name="bank%d" % r)
-            for c in range(4):
-                a = 4 * r + c
-                nc.tensor.transpose(
-                    spread[:, c * P : (c + 1) * P], gate_cols[:, a : a + 1].to_broadcast([P, P]), ident[:]
-                )
-            nc.scalar.copy(gate_sb[r][:], spread[:])
-
-        gather_bytes(0, 256)
-        gather_words(0, 128)
-        gather_words(128, 256)
-        for j in range(256, S, 256):
-            gather_bytes(j, j + 256)
-            gather_words(j, j + 256)
+            nc.sync.dma_start(gate_sb[r][:], gate[r])
 
         h_words = {}
         banks = {}
@@ -179,7 +179,7 @@ def tile_moe_elr_gelu_kernel(
                     nc.tensor.matmul_mx(
                         banks[e][a][:, 0:half_h],
                         lhsT=x_slot[s][:, cols].bitcast(FP8X4),
-                        lhsT_scale=xs_slot[s][:, cols],
+                        lhsT_scale=xs_slot[0][X_ROW[s] : P, cols],
                         rhs=wa_sb[:, PASSES * e + s, hid].bitcast(FP8X4),
                         rhs_scale=was_sb[e // 4][WA_ROW[e // 4] : P, PASSES * (e % 4) + s, hid],
                         start=(s == 0),
@@ -199,10 +199,10 @@ def tile_moe_elr_gelu_kernel(
 
         def turn(e):
             words = h_words[e][:].bitcast(F32)
-            if e + 1 < E:
-                bank = banks[e + 1][1]
+            if e < 5:
+                bank = banks[e + 2][1]
             else:
-                bank = psum_h.tile([P, H], F32, name="bank1")
+                bank = psum_h.tile([P, H], F32, name="bank0")
             turned[e] = bank[:, half_h:H].rearrange("p (u j) -> p u j", u=2)
             for u in range(2):
                 nc.tensor.transpose(turned[e][:, u, :], words[:, u * P : (u + 1) * P], ident[:])
@@ -251,20 +251,26 @@ def tile_moe_elr_gelu_kernel(
                 )
             evacuate(y_sb[:, e0 * C : e1 * C], y[:, 0 : (e1 - e0) * C])
 
-        for step in range(E + 1):
-            if step < E:
-                first_layer(step)
-                activate(step, 0)
-            if step >= 1:
-                turn(step - 1)
-            if step < E:
-                activate(step, 1)
-            if step >= 1:
-                regroup(step - 1)
-            if step in (2, 4, 6):
-                quantise(step - 2, step)
-            if step >= 7:
-                quantise(step - 1, step)
+        for e in range(E - 1):
+            first_layer(e)
+            activate(e, 0)
+            if e >= 2:
+                turn(e - 2)
+            activate(e, 1)
+            if e >= 2:
+                regroup(e - 2)
+            if e in (3, 5):
+                quantise(e - 3, e - 1)
+        turn(5)
+        regroup(5)
+        quantise(4, 6)
+        first_layer(7)
+        activate(7, 0)
+        activate(7, 1)
+        for e in (6, 7):
+            turn(e)
+            regroup(e)
+            quantise(e, e + 1)
         second_layer(0, 4, nc.vector.tensor_copy)
         second_layer(4, 7, nc.vector.tensor_copy)
         second_layer(7, 8, nc.scalar.copy)

@@ -23,7 +23,6 @@ ADD = mybir.AluOpType.add
 FLOPS = 2 * S * (K * H + K * N + H * N)
 
 X_ROW = (0, 4)
-WA_ROW = (12, 4)
 WB_ROW = 8
 
 
@@ -44,7 +43,7 @@ def tile_moe_elr_gelu_kernel(
         x_slot = [keep.tile([P, S], I32, name="x_slot%d" % s, align_bytes=64) for s in range(PASSES)]
         xs_slot = [keep.tile([P, S], U8, name="xs_slot%d" % s, align_bytes=64) for s in range(PASSES)]
         wa_sb = keep.tile([P, E * PASSES, H], I32, name="wa_sb", align_bytes=64)
-        was_sb = [keep.tile([P, E // 2 * PASSES, H], U8, name="was_sb%d" % g, align_bytes=64) for g in range(2)]
+        was_sb = keep.tile([P, E // 2, H], U8, name="was_sb", align_bytes=64)
         w_sb = keep.tile([P, E * PASSES, 2 * N], U8, name="w_sb", align_bytes=64)
         ws_sb = keep.tile([P, E * PASSES, N], U8, name="ws_sb", align_bytes=64)
         wb_sb = keep.tile([P, E, N], I32, name="wb_sb", align_bytes=64)
@@ -72,23 +71,21 @@ def tile_moe_elr_gelu_kernel(
             )
 
         def load_was(queue, g, q):
-            row = 32 * q + WA_ROW[g]
             queue.dma_start(
-                was_sb[g][row : row + 4, :, :].bitcast(I32),
-                wa_scales[4 * g : 4 * g + 4, :, 4 * q : 4 * q + 4, :].rearrange("e s r i -> r (e s) i").bitcast(I32),
+                was_sb[32 * q : 32 * q + 16, g, :].bitcast(I32),
+                wa_scales[2 * g : 2 * g + 2, :, 4 * q : 4 * q + 4, :].rearrange("e s r i -> (e s) r i").bitcast(I32),
             )
 
-        def load_ws(queue, q):
+        def load_ws(queue, r):
             queue.dma_start(
-                ws_sb[32 * q : 32 * q + 4, :, :].bitcast(I32),
-                w_scales[:, :, 4 * q : 4 * q + 4, :].rearrange("e s r n -> r (e s) n").bitcast(I32),
+                ws_sb[r:P:32, :, :].bitcast(I32),
+                w_scales.rearrange("e s (q r) n -> r q (e s) n", r=4)[r].bitcast(I32),
             )
 
-        def load_wbs(queue, q):
-            row = 32 * q + WB_ROW
+        def load_wbs(queue, r):
             queue.dma_start(
-                wbs_sb[row : row + 4, :, :].bitcast(I32),
-                wb_scales[:, 0, 4 * q : 4 * q + 4, :].rearrange("e r n -> r e n").bitcast(I32),
+                wbs_sb[WB_ROW + r : P : 32, :, :].bitcast(I32),
+                wb_scales.rearrange("e o (q r) n -> r q (e o) n", r=4)[r].bitcast(I32),
             )
 
         def gather_bytes(j0, j1):
@@ -107,15 +104,12 @@ def tile_moe_elr_gelu_kernel(
 
         make_identity(nc, ident[:])
         for q in range(4):
-            load_ws(nc.gpsimd, q)
-        for q in range(2):
-            load_wbs(nc.gpsimd, q)
+            load_was(nc.gpsimd, 3, q)
+        for r in range(4):
+            load_ws(nc.gpsimd, r)
 
-        def move_scales(q):
-            nc.sync.dma_start(
-                xs_slot[1][32 * q : 32 * q + 4, :].bitcast(I32),
-                xs_slot[0][32 * q + 4 : 32 * q + 8, :].bitcast(I32),
-            )
+        def move_scales(r):
+            nc.sync.dma_start(xs_slot[1][r:P:32, :].bitcast(I32), xs_slot[0][4 + r : P : 32, :].bitcast(I32))
 
         nc.sync.dma_start(offs_sb[:], offs)
         for q in range(4):
@@ -132,6 +126,11 @@ def tile_moe_elr_gelu_kernel(
         for q in range(4):
             load_was(nc.sync, 1, q)
         load_wa(nc.sync, 3, 4)
+        load_was(nc.sync, 2, 0)
+        load_was(nc.sync, 2, 1)
+        load_wa(nc.sync, 4, 5)
+        load_was(nc.sync, 2, 2)
+        load_was(nc.sync, 2, 3)
         load_w(0, 4)
 
         gather_bytes(0, 256)
@@ -144,14 +143,15 @@ def tile_moe_elr_gelu_kernel(
 
         move_scales(0)
         move_scales(1)
-        load_wa(nc.sync, 4, 5)
+        load_wa(nc.sync, 5, 6)
         move_scales(2)
         move_scales(3)
-        load_wa(nc.sync, 5, 6)
+        load_wa(nc.sync, 6, 7)
+        load_wbs(nc.sync, 0)
+        load_wbs(nc.sync, 1)
+        load_wb(0, 4)
         load_wbs(nc.sync, 2)
         load_wbs(nc.sync, 3)
-        load_wa(nc.sync, 6, 7)
-        load_wb(0, 4)
         for a in range(2):
             nc.sync.dma_start(
                 wa_sb[:, PASSES * (E - 1) :, a * (H // 2) : (a + 1) * (H // 2)],
@@ -181,7 +181,7 @@ def tile_moe_elr_gelu_kernel(
                         lhsT=x_slot[s][:, cols].bitcast(FP8X4),
                         lhsT_scale=xs_slot[0][X_ROW[s] : P, cols],
                         rhs=wa_sb[:, PASSES * e + s, hid].bitcast(FP8X4),
-                        rhs_scale=was_sb[e // 4][WA_ROW[e // 4] : P, PASSES * (e % 4) + s, hid],
+                        rhs_scale=was_sb[4 * (PASSES * (e % 2) + s) : P, e // 2, hid],
                         start=(s == 0),
                         stop=(s == PASSES - 1),
                     )

@@ -24,6 +24,7 @@ FLOPS = 2 * S * (K * H + K * N + H * N)
 
 X_ROW = (0, 4)
 WB_ROW = 8
+GROUPS = ((0, 4), (6, 7), (4, 6), (7, 8))
 
 
 def tile_moe_elr_gelu_kernel(
@@ -34,41 +35,27 @@ def tile_moe_elr_gelu_kernel(
         keep = ctx.enter_context(tc.tile_pool(name="keep", bufs=1))
         ring = ctx.enter_context(tc.tile_pool(name="ring", bufs=4))
         psum_h = ctx.enter_context(tc.psum_pool(name="psum_h", bufs=3))
-        psum_y = ctx.enter_context(tc.psum_pool(name="psum_y", bufs=2))
+        psum = ctx.enter_context(tc.psum_pool(name="psum", bufs=1))
 
         offs_sb = keep.tile([P, S // 16], U16, name="offs_sb")
         pos_sb = [keep.tile([P, T // 16], U16, name="pos%d_sb" % r) for r in range(2)]
-        x_tok = keep.tile([P, PASSES, T], I32, name="x_tok", align_bytes=64)
-        xs_tok = keep.tile([P, T], U8, name="xs_tok", align_bytes=64)
-        x_slot = [keep.tile([P, S], I32, name="x_slot%d" % s, align_bytes=64) for s in range(PASSES)]
-        xs_slot = [keep.tile([P, S], U8, name="xs_slot%d" % s, align_bytes=64) for s in range(PASSES)]
-        wa_sb = keep.tile([P, E * PASSES, H], I32, name="wa_sb", align_bytes=64)
-        was_sb = keep.tile([P, E // 2, H], U8, name="was_sb", align_bytes=64)
-        w_sb = keep.tile([P, E * PASSES, 2 * N], U8, name="w_sb", align_bytes=64)
-        ws_sb = keep.tile([P, E * PASSES, N], U8, name="ws_sb", align_bytes=64)
-        wb_sb = keep.tile([P, E, N], I32, name="wb_sb", align_bytes=64)
-        wbs_sb = keep.tile([P, E, N], U8, name="wbs_sb", align_bytes=64)
+        x_tok = keep.tile([P, PASSES, T], I32, name="x_tok", align_bytes=256)
+        xs_tok = keep.tile([P, T], U8, name="xs_tok", align_bytes=256)
+        x_slot = [keep.tile([P, S], I32, name="x_slot%d" % s, align_bytes=256) for s in range(PASSES)]
+        xs_slot = [keep.tile([P, S], U8, name="xs_slot%d" % s, align_bytes=256) for s in range(PASSES)]
+        wa_sb = keep.tile([P, E * PASSES, H], I32, name="wa_sb", align_bytes=256)
+        was_sb = keep.tile([P, E // 2, H], U8, name="was_sb", align_bytes=256)
+        w_sb = [
+            keep.tile([P, (e1 - e0) * PASSES, 2 * N], U8, name="w_sb%d" % e0, align_bytes=256) for e0, e1 in GROUPS
+        ]
+        ws_sb = keep.tile([P, E * PASSES, N], U8, name="ws_sb", align_bytes=256)
+        wb_sb = [keep.tile([P, e1 - e0, N], I32, name="wb_sb%d" % e0, align_bytes=256) for e0, e1 in GROUPS]
+        wbs_sb = keep.tile([P, E, N], U8, name="wbs_sb", align_bytes=256)
+        gate_col = keep.tile([P, 2, 8], F32, name="gate_col")
         gate_sb = [keep.tile([P, T], F32, name="gate%d_sb" % r) for r in range(2)]
+        warm = keep.tile([P, 2], F32, name="warm")
         ident = keep.tile([P, P], F32, name="ident")
         y_sb = keep.tile([P, S], F32, name="y_sb")
-        warm = keep.tile([P, 2], F32, name="warm")
-
-        def load_wa(queue, e0, e1):
-            queue.dma_start(
-                wa_sb[:, PASSES * e0 : PASSES * e1, :],
-                wa_words[e0:e1].rearrange("e s p i d -> p (e s) (i d)").bitcast(I32),
-            )
-
-        def load_w(e0, e1):
-            nc.sync.dma_start(
-                w_sb[:, PASSES * e0 : PASSES * e1, :].bitcast(I32),
-                w_words[e0:e1].rearrange("e s p b -> p (e s) b").bitcast(I32),
-            )
-
-        def load_wb(e0, e1):
-            nc.sync.dma_start(
-                wb_sb[:, e0:e1, :], wb_words[e0:e1].rearrange("e o p n d -> p (e o) (n d)").bitcast(I32)
-            )
 
         def load_was(queue, g, q):
             queue.dma_start(
@@ -76,17 +63,30 @@ def tile_moe_elr_gelu_kernel(
                 wa_scales[2 * g : 2 * g + 2, :, 4 * q : 4 * q + 4, :].rearrange("e s r i -> (e s) r i").bitcast(I32),
             )
 
-        def load_ws(queue, r):
+        def load_wa(e, queue=nc.sync):
             queue.dma_start(
-                ws_sb[r:P:32, :, :].bitcast(I32),
-                w_scales.rearrange("e s (q r) n -> r q (e s) n", r=4)[r].bitcast(I32),
+                wa_sb[:, PASSES * e : PASSES * (e + 1), :],
+                wa_words[e].rearrange("s p i d -> p s (i d)").bitcast(I32),
             )
 
-        def load_wbs(queue, r):
-            queue.dma_start(
-                wbs_sb[WB_ROW + r : P : 32, :, :].bitcast(I32),
-                wb_scales.rearrange("e o (q r) n -> r q (e o) n", r=4)[r].bitcast(I32),
+        def load_second(g):
+            e0, e1 = GROUPS[g]
+            nc.sync.dma_start(
+                wb_sb[g][:], wb_words.rearrange("e o p n d -> p (e o) (n d)").bitcast(I32)[:, e0:e1, :]
             )
+            nc.sync.dma_start(
+                w_sb[g][:].bitcast(I32),
+                w_words.rearrange("e s p b -> p (e s) b").bitcast(I32)[:, PASSES * e0 : PASSES * e1, :],
+            )
+
+        def load_scales(queue, plane, first_row, scales, r):
+            queue.dma_start(
+                plane[first_row + r : P : 32, :, :].bitcast(I32),
+                scales.rearrange("e s (q r) n -> r q (e s) n", r=4)[r].bitcast(I32),
+            )
+
+        def move_scales(r):
+            nc.sync.dma_start(xs_slot[1][r:P:32, :].bitcast(I32), xs_slot[0][4 + r : P : 32, :].bitcast(I32))
 
         def gather_bytes(j0, j1):
             nc.vector.tensor_copy(xs_slot[0][:, j0:j1], xs_tok[:].indirect(offs_sb[:, j0 // 16 : j1 // 16]))
@@ -98,76 +98,70 @@ def tile_moe_elr_gelu_kernel(
                     x_tok[:, s, :].bitcast(U32).indirect(offs_sb[:, j0 // 16 : j1 // 16]),
                 )
 
+        load_wa(0, nc.scalar)
         nc.vector.memset(xs_tok[:].bitcast(I32), 0)
+        nc.vector.memset(ident[:], 0.0)
         nc.vector.memset(warm[:, 0:1], 0.0)
         nc.scalar.activation(warm[:, 1:2], warm[:, 0:1], GELU)
 
-        make_identity(nc, ident[:])
-        for q in range(4):
-            load_was(nc.gpsimd, 3, q)
+        make_identity(nc, ident[:], nomemset=True)
         for r in range(4):
-            load_ws(nc.gpsimd, r)
-
-        def move_scales(r):
-            nc.sync.dma_start(xs_slot[1][r:P:32, :].bitcast(I32), xs_slot[0][4 + r : P : 32, :].bitcast(I32))
+            load_scales(nc.gpsimd, wbs_sb, WB_ROW, wb_scales, r)
+        for r in range(4):
+            load_scales(nc.gpsimd, ws_sb, 0, w_scales, r)
 
         nc.sync.dma_start(offs_sb[:], offs)
         for q in range(4):
             nc.sync.dma_start(
                 xs_tok[32 * q : 32 * q + 8, :].bitcast(I32), x_scales[:, 4 * q : 4 * q + 4, :].bitcast(I32)
             )
+        nc.sync.dma_start(gate_col[:, :, 0:4], gate[:, 0, :].rearrange("r (p j) -> p r j", j=4))
         nc.sync.dma_start(x_tok[:], x_words.rearrange("s p t d -> p s (t d)").bitcast(I32))
-        load_was(nc.sync, 0, 0)
-        load_wa(nc.sync, 0, 1)
-        for q in range(1, 4):
-            load_was(nc.sync, 0, q)
-        load_wa(nc.sync, 1, 2)
-        load_wa(nc.sync, 2, 3)
         for q in range(4):
-            load_was(nc.sync, 1, q)
-        load_wa(nc.sync, 3, 4)
-        load_was(nc.sync, 2, 0)
-        load_was(nc.sync, 2, 1)
-        load_wa(nc.sync, 4, 5)
-        load_was(nc.sync, 2, 2)
-        load_was(nc.sync, 2, 3)
-        load_w(0, 4)
+            load_was(nc.sync, 0, q)
 
-        gather_bytes(0, 256)
+        def load_expert(e):
+            load_wa(e)
+            for q in range(2):
+                load_was(nc.sync, (e + 1) // 2, 2 * ((e + 1) % 2) + q)
+
+        load_expert(1)
+        load_expert(2)
+        nc.sync.dma_start(pos_sb[0][:], pos1)
+        load_expert(3)
+        nc.sync.dma_start(pos_sb[1][:], pos2)
+        load_expert(4)
+
+        gather_bytes(0, 384)
+        gather_bytes(384, 768)
+        gather_bytes(768, S)
         gather_words(0, 128)
         gather_words(128, 256)
-        gather_bytes(256, 640)
-        gather_bytes(640, 1024)
         for j in range(256, S, 256):
             gather_words(j, j + 256)
 
-        move_scales(0)
-        move_scales(1)
-        load_wa(nc.sync, 5, 6)
+        for e in (5, 6):
+            load_expert(e)
+            move_scales(e - 5)
+        load_wa(7)
         move_scales(2)
         move_scales(3)
-        load_wa(nc.sync, 6, 7)
-        load_wbs(nc.sync, 0)
-        load_wbs(nc.sync, 1)
-        load_wb(0, 4)
-        load_wbs(nc.sync, 2)
-        load_wbs(nc.sync, 3)
-        for a in range(2):
-            nc.sync.dma_start(
-                wa_sb[:, PASSES * (E - 1) :, a * (H // 2) : (a + 1) * (H // 2)],
-                wa_words[E - 1, :, :, a * (H // 2) : (a + 1) * (H // 2), :]
-                .rearrange("s p i d -> p s (i d)")
-                .bitcast(I32),
-            )
-        load_w(4, E)
-        load_wb(4, E)
-        nc.sync.dma_start(pos_sb[0][:], pos1)
-        nc.sync.dma_start(pos_sb[1][:], pos2)
+        for g in range(len(GROUPS)):
+            load_second(g)
+
         for r in range(2):
-            nc.sync.dma_start(gate_sb[r][:], gate[r])
+            bank = psum.tile([P, 4, P], F32, name="spare%d" % r)
+            for j in range(4):
+                nc.tensor.transpose(bank[:, j, :], gate_col[:, r, j : j + 1].to_broadcast([P, P]), ident[:])
+            nc.scalar.copy(gate_sb[r][:].rearrange("p (n j) -> p n j", j=4), bank[:].rearrange("p j n -> p n j"))
 
         h_words = {}
+        grouped = [keep.tile([P, 2 * 4 * C], BF16, name="grouped%d" % a, align_bytes=256) for a in range(E // 2)]
+        h_codes = keep.tile([P, S], U32, name="h_codes", align_bytes=256)
+        h_scales = keep.tile([P, S], U8, name="h_scales", align_bytes=256)
+
         banks = {}
+        turned = {}
         half_h = H // 2
 
         def first_layer(e):
@@ -188,32 +182,22 @@ def tile_moe_elr_gelu_kernel(
 
         def activate(e, a):
             if a == 0:
-                h_words[e] = ring.tile([P, H], BF16, name="h", align_bytes=64)
+                h_words[e] = ring.tile([P, H], BF16, name="h", align_bytes=256)
             nc.scalar.activation(
                 h_words[e][:].rearrange("j (u p b) -> j u p b", u=2, b=2)[:, :, 64 * a : 64 * (a + 1), :],
                 banks[e][a][:, 0:half_h].rearrange("j (p u b) -> j u p b", u=2, b=2),
                 GELU,
             )
 
-        turned = {}
-
-        def turn(e):
+        def turn(e, bank):
             words = h_words[e][:].bitcast(F32)
-            if e < 5:
-                bank = banks[e + 2][1]
-            else:
-                bank = psum_h.tile([P, H], F32, name="bank0")
             turned[e] = bank[:, half_h:H].rearrange("p (u j) -> p u j", u=2)
             for u in range(2):
                 nc.tensor.transpose(turned[e][:, u, :], words[:, u * P : (u + 1) * P], ident[:])
 
-        grouped = keep.tile([P, E, 4 * C], BF16, name="grouped", align_bytes=64)
-        h_codes = keep.tile([P, S], U32, name="h_codes", align_bytes=64)
-        h_scales = keep.tile([P, S], U8, name="h_scales", align_bytes=64)
-
-        def regroup(e):
-            nc.scalar.copy(
-                grouped[:, e, :].bitcast(F32).rearrange("p (j u) -> p j u", u=2),
+        def regroup(e, copy):
+            copy(
+                grouped[e // 2][:].bitcast(F32).rearrange("p (e j u) -> p e j u", e=2, u=2)[:, e % 2],
                 turned[e].rearrange("p u j -> p j u"),
             )
 
@@ -222,58 +206,57 @@ def tile_moe_elr_gelu_kernel(
             nc.vector.quantize_mx(
                 h_codes[:, cols].bitcast(FP8X4),
                 h_scales[:, cols],
-                grouped[:, e0:e1, :].rearrange("p e f -> p (e f)"),
+                grouped[e0 // 2][:],
             )
 
-        def second_layer(e0, e1, evacuate):
-            y = psum_y.tile([P, T], F32, name="y")
-            for e in range(e0, e1):
+        def second_layer(order, pool, tag, evacuate):
+            first = min(order)
+            y = pool.tile([P, 4, P], F32, name=tag)
+            for e in order:
+                g = [k for k, (e0, e1) in enumerate(GROUPS) if e0 <= e < e1][0]
+                at = e - GROUPS[g][0]
                 cols = slice(e * C, (e + 1) * C)
-                acc = y[:, (e - e0) * C : (e - e0 + 1) * C]
-                for s in range(PASSES):
-                    nc.tensor.matmul_mx(
-                        acc,
-                        lhsT=w_sb[:, PASSES * e + s, :].bitcast(FP4X4),
-                        lhsT_scale=ws_sb[:, PASSES * e + s, :],
-                        rhs=x_slot[s][:, cols].bitcast(FP8X4),
-                        rhs_scale=xs_slot[s][:, cols],
-                        start=(s == 0),
-                        stop=False,
-                    )
+                acc = y[:, e - first, :]
                 nc.tensor.matmul_mx(
                     acc,
-                    lhsT=wb_sb[:, e, :].bitcast(FP8X4),
+                    lhsT=wb_sb[g][:, at, :].bitcast(FP8X4),
                     lhsT_scale=wbs_sb[WB_ROW:P, e, :],
                     rhs=h_codes[:, cols].bitcast(FP8X4),
                     rhs_scale=h_scales[:, cols],
-                    start=False,
-                    stop=True,
+                    start=True,
+                    stop=False,
                 )
-            evacuate(y_sb[:, e0 * C : e1 * C], y[:, 0 : (e1 - e0) * C])
+                for s in range(PASSES):
+                    nc.tensor.matmul_mx(
+                        acc,
+                        lhsT=w_sb[g][:, PASSES * at + s, :].bitcast(FP4X4),
+                        lhsT_scale=ws_sb[:, PASSES * e + s, :],
+                        rhs=x_slot[s][:, cols].bitcast(FP8X4),
+                        rhs_scale=xs_slot[s][:, cols],
+                        start=False,
+                        stop=(s == PASSES - 1),
+                    )
+            n = len(order)
+            evacuate(y_sb[:, first * C : (first + n) * C], y[:, 0:n, :].rearrange("p e j -> p (e j)"))
 
-        for e in range(E - 1):
+        for e in range(E):
             first_layer(e)
             activate(e, 0)
             if e >= 2:
-                turn(e - 2)
+                turn(e - 2, banks[e][1])
             activate(e, 1)
             if e >= 2:
-                regroup(e - 2)
-            if e in (3, 5):
+                regroup(e - 2, nc.scalar.copy if e < 6 else nc.vector.tensor_copy)
+            if e in (3, 5, 7):
                 quantise(e - 3, e - 1)
-        turn(5)
-        regroup(5)
-        quantise(4, 6)
-        first_layer(7)
-        activate(7, 0)
-        activate(7, 1)
-        for e in (6, 7):
-            turn(e)
-            regroup(e)
-            quantise(e, e + 1)
-        second_layer(0, 4, nc.vector.tensor_copy)
-        second_layer(4, 7, nc.vector.tensor_copy)
-        second_layer(7, 8, nc.scalar.copy)
+        turn(6, banks[7][0])
+        regroup(6, nc.vector.tensor_copy)
+        turn(7, psum.tile([P, H], F32, name="spare0"))
+        regroup(7, nc.scalar.copy)
+        quantise(6, 8)
+        second_layer((0, 1, 2, 3), psum, "spare0", nc.scalar.copy)
+        second_layer((6, 4, 5), psum, "spare1", nc.vector.tensor_copy)
+        second_layer((7,), psum_h, "bank0", nc.scalar.copy)
 
         half = T // 2
         prod = [keep.tile([P, T], F32, name="prod%d" % r) for r in range(2)]

@@ -1,7 +1,6 @@
 from contextlib import ExitStack
 
 import concourse.mybir as mybir
-from concourse.masks import make_identity
 
 K, T, E, C, H, N = 1024, 512, 8, 128, 512, 128
 S = E * C
@@ -48,7 +47,6 @@ def tile_moe_elr_gelu_kernel(
         w_sb = [
             keep.tile([P, (e1 - e0) * PASSES, 2 * N], U8, name="w_sb%d" % e0, align_bytes=256) for e0, e1 in GROUPS
         ]
-        ws_sb = keep.tile([P, E * PASSES, N], U8, name="ws_sb", align_bytes=256)
         wb_sb = [keep.tile([P, e1 - e0, N], I32, name="wb_sb%d" % e0, align_bytes=256) for e0, e1 in GROUPS]
         wbs_sb = keep.tile([P, E, N], U8, name="wbs_sb", align_bytes=256)
         gate_col = keep.tile([P, 2, 8], F32, name="gate_col")
@@ -69,11 +67,14 @@ def tile_moe_elr_gelu_kernel(
                 wa_words[e].rearrange("s p i d -> p s (i d)").bitcast(I32),
             )
 
-        def load_second(g):
+        def load_wb(g):
             e0, e1 = GROUPS[g]
             nc.sync.dma_start(
                 wb_sb[g][:], wb_words.rearrange("e o p n d -> p (e o) (n d)").bitcast(I32)[:, e0:e1, :]
             )
+
+        def load_w(g):
+            e0, e1 = GROUPS[g]
             nc.sync.dma_start(
                 w_sb[g][:].bitcast(I32),
                 w_words.rearrange("e s p b -> p (e s) b").bitcast(I32)[:, PASSES * e0 : PASSES * e1, :],
@@ -100,13 +101,21 @@ def tile_moe_elr_gelu_kernel(
 
         load_wa(0, nc.scalar)
         nc.vector.memset(xs_tok[:].bitcast(I32), 0)
-        nc.vector.memset(ident[:], 0.0)
         nc.vector.memset(warm[:, 0:1], 0.0)
         nc.scalar.activation(warm[:, 1:2], warm[:, 0:1], GELU)
 
-        make_identity(nc, ident[:], nomemset=True)
-        for r in range(4):
-            load_scales(nc.gpsimd, wbs_sb, WB_ROW, wb_scales, r)
+        zeros = keep.tile([P, P], F32, name="ws_sb", align_bytes=256)
+        nc.gpsimd.memset(zeros[:], 0.0)
+        nc.gpsimd.affine_select(
+            out=ident[:],
+            in_=zeros[:],
+            compare_op=mybir.AluOpType.not_equal,
+            fill=1.0,
+            base=0,
+            pattern=[[-1, P]],
+            channel_multiplier=1,
+        )
+        ws_sb = keep.tile([P, E * PASSES, N], U8, name="ws_sb", align_bytes=256)
         for r in range(4):
             load_scales(nc.gpsimd, ws_sb, 0, w_scales, r)
 
@@ -125,12 +134,9 @@ def tile_moe_elr_gelu_kernel(
             for q in range(2):
                 load_was(nc.sync, (e + 1) // 2, 2 * ((e + 1) % 2) + q)
 
-        load_expert(1)
-        load_expert(2)
-        nc.sync.dma_start(pos_sb[0][:], pos1)
-        load_expert(3)
-        nc.sync.dma_start(pos_sb[1][:], pos2)
-        load_expert(4)
+        for e in range(1, E - 1):
+            load_expert(e)
+        load_wa(E - 1)
 
         gather_bytes(0, 384)
         gather_bytes(384, 768)
@@ -140,14 +146,21 @@ def tile_moe_elr_gelu_kernel(
         for j in range(256, S, 256):
             gather_words(j, j + 256)
 
-        for e in (5, 6):
-            load_expert(e)
-            move_scales(e - 5)
-        load_wa(7)
-        move_scales(2)
-        move_scales(3)
-        for g in range(len(GROUPS)):
-            load_second(g)
+        for r in range(4):
+            load_scales(nc.sync, wbs_sb, WB_ROW, wb_scales, r)
+            if r == 1:
+                load_wb(0)
+        for r in range(4):
+            move_scales(r)
+            if r == 1:
+                load_w(0)
+        for g in (1, 2):
+            load_wb(g)
+            load_w(g)
+        nc.sync.dma_start(pos_sb[0][:], pos1)
+        nc.sync.dma_start(pos_sb[1][:], pos2)
+        load_wb(3)
+        load_w(3)
 
         for r in range(2):
             bank = psum.tile([P, 4, P], F32, name="spare%d" % r)

@@ -23,7 +23,8 @@ FLOPS = 2 * S * (K * H + K * N + H * N)
 
 X_ROW = (0, 4)
 WB_ROW = 8
-GROUPS = ((0, 4), (6, 7), (4, 6), (7, 8))
+WA_ROW = 12
+GROUPS = ((0, 2), (2, 5), (5, 7), (7, 8))
 
 
 def tile_moe_elr_gelu_kernel(
@@ -43,28 +44,21 @@ def tile_moe_elr_gelu_kernel(
         x_slot = [keep.tile([P, S], I32, name="x_slot%d" % s, align_bytes=256) for s in range(PASSES)]
         xs_slot = [keep.tile([P, S], U8, name="xs_slot%d" % s, align_bytes=256) for s in range(PASSES)]
         wa_sb = keep.tile([P, E * PASSES, H], I32, name="wa_sb", align_bytes=256)
-        was_sb = keep.tile([P, E // 2, H], U8, name="was_sb", align_bytes=256)
+        was_sb = keep.tile([P, E * PASSES, H], U8, name="was_sb", align_bytes=256)
         w_sb = [
             keep.tile([P, (e1 - e0) * PASSES, 2 * N], U8, name="w_sb%d" % e0, align_bytes=256) for e0, e1 in GROUPS
         ]
         wb_sb = [keep.tile([P, e1 - e0, N], I32, name="wb_sb%d" % e0, align_bytes=256) for e0, e1 in GROUPS]
-        wbs_sb = keep.tile([P, E, N], U8, name="wbs_sb", align_bytes=256)
         gate_col = keep.tile([P, 2, 8], F32, name="gate_col")
         gate_sb = [keep.tile([P, T], F32, name="gate%d_sb" % r) for r in range(2)]
         warm = keep.tile([P, 2], F32, name="warm")
         ident = keep.tile([P, P], F32, name="ident")
         y_sb = keep.tile([P, S], F32, name="y_sb")
 
-        def load_was(queue, g, q):
-            queue.dma_start(
-                was_sb[32 * q : 32 * q + 16, g, :].bitcast(I32),
-                wa_scales[2 * g : 2 * g + 2, :, 4 * q : 4 * q + 4, :].rearrange("e s r i -> (e s) r i").bitcast(I32),
-            )
-
-        def load_wa(e, queue=nc.sync):
-            queue.dma_start(
-                wa_sb[:, PASSES * e : PASSES * (e + 1), :],
-                wa_words[e].rearrange("s p i d -> p s (i d)").bitcast(I32),
+        def load_wa(e0, e1, hid=slice(0, H)):
+            nc.sync.dma_start(
+                wa_sb[:, PASSES * e0 : PASSES * e1, hid],
+                wa_words.rearrange("e s p i d -> p (e s) (i d)").bitcast(I32)[:, PASSES * e0 : PASSES * e1, hid],
             )
 
         def load_wb(g):
@@ -99,7 +93,6 @@ def tile_moe_elr_gelu_kernel(
                     x_tok[:, s, :].bitcast(U32).indirect(offs_sb[:, j0 // 16 : j1 // 16]),
                 )
 
-        load_wa(0, nc.scalar)
         nc.vector.memset(xs_tok[:].bitcast(I32), 0)
         nc.vector.memset(warm[:, 0:1], 0.0)
         nc.scalar.activation(warm[:, 1:2], warm[:, 0:1], GELU)
@@ -117,6 +110,8 @@ def tile_moe_elr_gelu_kernel(
         )
         ws_sb = keep.tile([P, E * PASSES, N], U8, name="ws_sb", align_bytes=256)
         for r in range(4):
+            load_scales(nc.gpsimd, ws_sb[:, 0:E, :], WB_ROW, wb_scales, r)
+        for r in range(4):
             load_scales(nc.gpsimd, ws_sb, 0, w_scales, r)
 
         nc.sync.dma_start(offs_sb[:], offs)
@@ -126,17 +121,11 @@ def tile_moe_elr_gelu_kernel(
             )
         nc.sync.dma_start(gate_col[:, :, 0:4], gate[:, 0, :].rearrange("r (p j) -> p r j", j=4))
         nc.sync.dma_start(x_tok[:], x_words.rearrange("s p t d -> p s (t d)").bitcast(I32))
-        for q in range(4):
-            load_was(nc.sync, 0, q)
-
-        def load_expert(e):
-            load_wa(e)
-            for q in range(2):
-                load_was(nc.sync, (e + 1) // 2, 2 * ((e + 1) % 2) + q)
-
-        for e in range(1, E - 1):
-            load_expert(e)
-        load_wa(E - 1)
+        for r in range(4):
+            load_scales(nc.sync, was_sb, WA_ROW, wa_scales, r)
+        load_wa(0, 1)
+        load_wa(1, 3)
+        load_wa(3, 5)
 
         gather_bytes(0, 384)
         gather_bytes(384, 768)
@@ -146,21 +135,17 @@ def tile_moe_elr_gelu_kernel(
         for j in range(256, S, 256):
             gather_words(j, j + 256)
 
-        for r in range(4):
-            load_scales(nc.sync, wbs_sb, WB_ROW, wb_scales, r)
-            if r == 1:
-                load_wb(0)
-        for r in range(4):
-            move_scales(r)
-            if r == 1:
-                load_w(0)
-        for g in (1, 2):
+        for e in (5, 6):
+            load_wa(e, e + 1)
+            for r in (2 * e - 10, 2 * e - 9):
+                move_scales(r)
+        for a in range(2):
+            load_wa(7, 8, hid=slice(a * H // 2, (a + 1) * H // 2))
+        for g in range(len(GROUPS)):
             load_wb(g)
             load_w(g)
-        nc.sync.dma_start(pos_sb[0][:], pos1)
-        nc.sync.dma_start(pos_sb[1][:], pos2)
-        load_wb(3)
-        load_w(3)
+            if g < 2:
+                nc.sync.dma_start(pos_sb[g][:], (pos1, pos2)[g])
 
         for r in range(2):
             bank = psum.tile([P, 4, P], F32, name="spare%d" % r)
@@ -188,7 +173,7 @@ def tile_moe_elr_gelu_kernel(
                         lhsT=x_slot[s][:, cols].bitcast(FP8X4),
                         lhsT_scale=xs_slot[0][X_ROW[s] : P, cols],
                         rhs=wa_sb[:, PASSES * e + s, hid].bitcast(FP8X4),
-                        rhs_scale=was_sb[4 * (PASSES * (e % 2) + s) : P, e // 2, hid],
+                        rhs_scale=was_sb[WA_ROW:P, PASSES * e + s, hid],
                         start=(s == 0),
                         stop=(s == PASSES - 1),
                     )
@@ -219,7 +204,7 @@ def tile_moe_elr_gelu_kernel(
             nc.vector.quantize_mx(
                 h_codes[:, cols].bitcast(FP8X4),
                 h_scales[:, cols],
-                grouped[e0 // 2][:],
+                grouped[e0 // 2][:, (e0 % 2) * 4 * C : (e0 % 2 + e1 - e0) * 4 * C],
             )
 
         def second_layer(order, pool, tag, evacuate):
@@ -233,7 +218,7 @@ def tile_moe_elr_gelu_kernel(
                 nc.tensor.matmul_mx(
                     acc,
                     lhsT=wb_sb[g][:, at, :].bitcast(FP8X4),
-                    lhsT_scale=wbs_sb[WB_ROW:P, e, :],
+                    lhsT_scale=ws_sb[WB_ROW:P, e, :],
                     rhs=h_codes[:, cols].bitcast(FP8X4),
                     rhs_scale=h_scales[:, cols],
                     start=True,
@@ -252,7 +237,7 @@ def tile_moe_elr_gelu_kernel(
             n = len(order)
             evacuate(y_sb[:, first * C : (first + n) * C], y[:, 0:n, :].rearrange("p e j -> p (e j)"))
 
-        for e in range(E):
+        for e in range(E - 1):
             first_layer(e)
             activate(e, 0)
             if e >= 2:
@@ -260,38 +245,38 @@ def tile_moe_elr_gelu_kernel(
             activate(e, 1)
             if e >= 2:
                 regroup(e - 2, nc.scalar.copy if e < 6 else nc.vector.tensor_copy)
-            if e in (3, 5, 7):
+            if e in (3, 5):
                 quantise(e - 3, e - 1)
-        turn(6, banks[7][0])
-        regroup(6, nc.vector.tensor_copy)
-        turn(7, psum.tile([P, H], F32, name="spare0"))
+        turn(5, banks[6][0])
+        regroup(5, nc.vector.tensor_copy)
+        quantise(4, 6)
+        turn(6, psum.tile([P, H], F32, name="spare1"))
+        regroup(6, nc.scalar.copy)
+        quantise(6, 7)
+        first_layer(7)
+        activate(7, 0)
+        activate(7, 1)
+        second_layer((0, 1), psum, "spare0", nc.vector.tensor_copy)
+        turn(7, banks[7][1])
         regroup(7, nc.scalar.copy)
-        quantise(6, 8)
-        second_layer((0, 1, 2, 3), psum, "spare0", nc.scalar.copy)
-        second_layer((6, 4, 5), psum, "spare1", nc.vector.tensor_copy)
+        quantise(7, 8)
+        second_layer((2, 3, 4), psum, "spare1", nc.vector.tensor_copy)
+        second_layer((5, 6), psum, "spare0", nc.vector.tensor_copy)
         second_layer((7,), psum_h, "bank0", nc.scalar.copy)
 
         half = T // 2
         prod = [keep.tile([P, T], F32, name="prod%d" % r) for r in range(2)]
         res = [keep.tile([P, half], F32, name="res%d" % a) for a in range(2)]
 
-        def combine(r, a):
-            cols = slice(a * half, (a + 1) * half)
+        def combine(r, t0, t1):
             nc.vector.tensor_tensor(
-                prod[r][:, cols],
-                y_sb[:].indirect(pos_sb[r][:, a * half // 16 : (a + 1) * half // 16]),
-                gate_sb[r][:, cols],
-                MULT,
+                prod[r][:, t0:t1], y_sb[:].indirect(pos_sb[r][:, t0 // 16 : t1 // 16]), gate_sb[r][:, t0:t1], MULT
             )
 
-        def finish(a):
+        combine(0, 0, T)
+        combine(1, 0, half)
+        combine(1, half, T)
+        for a in range(2):
             cols = slice(a * half, (a + 1) * half)
             nc.vector.tensor_tensor(res[a][:], prod[0][:, cols], prod[1][:, cols], ADD)
             nc.sync.dma_start(out[:, cols], res[a][:])
-
-        combine(0, 0)
-        combine(1, 0)
-        combine(0, 1)
-        finish(0)
-        combine(1, 1)
-        finish(1)

@@ -23,7 +23,6 @@ FLOPS = 2 * S * (K * H + K * N + H * N)
 
 X_ROW = (0, 4)
 WB_ROW = 8
-WA_ROW = 12
 GROUPS = ((0, 2), (2, 5), (5, 7), (7, 8))
 
 
@@ -44,16 +43,21 @@ def tile_moe_elr_gelu_kernel(
         x_slot = [keep.tile([P, S], I32, name="x_slot%d" % s, align_bytes=256) for s in range(PASSES)]
         xs_slot = [keep.tile([P, S], U8, name="xs_slot%d" % s, align_bytes=256) for s in range(PASSES)]
         wa_sb = keep.tile([P, E * PASSES, H], I32, name="wa_sb", align_bytes=256)
-        was_sb = keep.tile([P, E * PASSES, H], U8, name="was_sb", align_bytes=256)
+        was_sb = keep.tile([P, E // 2, H], U8, name="was_sb", align_bytes=256)
         w_sb = [
             keep.tile([P, (e1 - e0) * PASSES, 2 * N], U8, name="w_sb%d" % e0, align_bytes=256) for e0, e1 in GROUPS
         ]
         wb_sb = [keep.tile([P, e1 - e0, N], I32, name="wb_sb%d" % e0, align_bytes=256) for e0, e1 in GROUPS]
-        gate_col = keep.tile([P, 2, 8], F32, name="gate_col")
         gate_sb = [keep.tile([P, T], F32, name="gate%d_sb" % r) for r in range(2)]
         warm = keep.tile([P, 2], F32, name="warm")
         ident = keep.tile([P, P], F32, name="ident")
         y_sb = keep.tile([P, S], F32, name="y_sb")
+
+        def load_was(g, q):
+            nc.sync.dma_start(
+                was_sb[32 * q : 32 * q + 16, g, :].bitcast(I32),
+                wa_scales[2 * g : 2 * g + 2, :, 4 * q : 4 * q + 4, :].rearrange("e s r i -> (e s) r i").bitcast(I32),
+            )
 
         def load_wa(e0, e1, hid=slice(0, H)):
             nc.sync.dma_start(
@@ -119,13 +123,12 @@ def tile_moe_elr_gelu_kernel(
             nc.sync.dma_start(
                 xs_tok[32 * q : 32 * q + 8, :].bitcast(I32), x_scales[:, 4 * q : 4 * q + 4, :].bitcast(I32)
             )
-        nc.sync.dma_start(gate_col[:, :, 0:4], gate[:, 0, :].rearrange("r (p j) -> p r j", j=4))
         nc.sync.dma_start(x_tok[:], x_words.rearrange("s p t d -> p s (t d)").bitcast(I32))
-        for r in range(4):
-            load_scales(nc.sync, was_sb, WA_ROW, wa_scales, r)
         load_wa(0, 1)
-        load_wa(1, 3)
-        load_wa(3, 5)
+        for g in range(3):
+            for q in range(4):
+                load_was(g, q)
+            load_wa(2 * g + 1, min(2 * g + 3, 6))
 
         gather_bytes(0, 384)
         gather_bytes(384, 768)
@@ -135,23 +138,23 @@ def tile_moe_elr_gelu_kernel(
         for j in range(256, S, 256):
             gather_words(j, j + 256)
 
-        for e in (5, 6):
-            load_wa(e, e + 1)
-            for r in (2 * e - 10, 2 * e - 9):
+        for a in range(2):
+            for q in (2 * a, 2 * a + 1):
+                load_was(3, q)
+            for r in (2 * a, 2 * a + 1):
                 move_scales(r)
+            if a == 0:
+                load_wa(6, 7)
         for a in range(2):
             load_wa(7, 8, hid=slice(a * H // 2, (a + 1) * H // 2))
-        for g in range(len(GROUPS)):
+        for g in range(len(GROUPS) - 1):
             load_wb(g)
             load_w(g)
-            if g < 2:
-                nc.sync.dma_start(pos_sb[g][:], (pos1, pos2)[g])
-
+        load_w(len(GROUPS) - 1)
+        load_wb(len(GROUPS) - 1)
         for r in range(2):
-            bank = psum.tile([P, 4, P], F32, name="spare%d" % r)
-            for j in range(4):
-                nc.tensor.transpose(bank[:, j, :], gate_col[:, r, j : j + 1].to_broadcast([P, P]), ident[:])
-            nc.scalar.copy(gate_sb[r][:].rearrange("p (n j) -> p n j", j=4), bank[:].rearrange("p j n -> p n j"))
+            nc.sync.dma_start(pos_sb[r][:], (pos1, pos2)[r])
+            nc.sync.dma_start(gate_sb[r][:], gate[r])
 
         h_words = {}
         grouped = [keep.tile([P, 2 * 4 * C], BF16, name="grouped%d" % a, align_bytes=256) for a in range(E // 2)]
@@ -173,7 +176,7 @@ def tile_moe_elr_gelu_kernel(
                         lhsT=x_slot[s][:, cols].bitcast(FP8X4),
                         lhsT_scale=xs_slot[0][X_ROW[s] : P, cols],
                         rhs=wa_sb[:, PASSES * e + s, hid].bitcast(FP8X4),
-                        rhs_scale=was_sb[WA_ROW:P, PASSES * e + s, hid],
+                        rhs_scale=was_sb[4 * (PASSES * (e % 2) + s) : P, e // 2, hid],
                         start=(s == 0),
                         stop=(s == PASSES - 1),
                     )
@@ -215,24 +218,29 @@ def tile_moe_elr_gelu_kernel(
                 at = e - GROUPS[g][0]
                 cols = slice(e * C, (e + 1) * C)
                 acc = y[:, e - first, :]
-                nc.tensor.matmul_mx(
-                    acc,
-                    lhsT=wb_sb[g][:, at, :].bitcast(FP8X4),
-                    lhsT_scale=ws_sb[WB_ROW:P, e, :],
-                    rhs=h_codes[:, cols].bitcast(FP8X4),
-                    rhs_scale=h_scales[:, cols],
-                    start=True,
-                    stop=False,
-                )
+                passes = [
+                    (wb_sb[g][:, at, :].bitcast(FP8X4), ws_sb[WB_ROW:P, e, :], h_codes[:, cols], h_scales[:, cols])
+                ]
                 for s in range(PASSES):
+                    passes.append(
+                        (
+                            w_sb[g][:, PASSES * at + s, :].bitcast(FP4X4),
+                            ws_sb[:, PASSES * e + s, :],
+                            x_slot[s][:, cols],
+                            xs_slot[s][:, cols],
+                        )
+                    )
+                if e == E - 1:
+                    passes = passes[1:] + passes[:1]
+                for k, (weights, weight_scales, words, scales) in enumerate(passes):
                     nc.tensor.matmul_mx(
                         acc,
-                        lhsT=w_sb[g][:, PASSES * at + s, :].bitcast(FP4X4),
-                        lhsT_scale=ws_sb[:, PASSES * e + s, :],
-                        rhs=x_slot[s][:, cols].bitcast(FP8X4),
-                        rhs_scale=xs_slot[s][:, cols],
-                        start=False,
-                        stop=(s == PASSES - 1),
+                        lhsT=weights,
+                        lhsT_scale=weight_scales,
+                        rhs=words.bitcast(FP8X4),
+                        rhs_scale=scales,
+                        start=(k == 0),
+                        stop=(k == len(passes) - 1),
                     )
             n = len(order)
             evacuate(y_sb[:, first * C : (first + n) * C], y[:, 0:n, :].rearrange("p e j -> p (e j)"))

@@ -23,7 +23,7 @@ FLOPS = 2 * S * (K * H + K * N + H * N)
 
 X_ROW = (0, 4)
 WB_ROW = 8
-GROUPS = ((0, 2), (2, 5), (5, 7), (7, 8))
+GROUPS = ((0, 3), (3, 6), (6, 8))
 
 
 def tile_moe_elr_gelu_kernel(
@@ -49,7 +49,6 @@ def tile_moe_elr_gelu_kernel(
         ]
         wb_sb = [keep.tile([P, e1 - e0, N], I32, name="wb_sb%d" % e0, align_bytes=256) for e0, e1 in GROUPS]
         gate_sb = [keep.tile([P, T], F32, name="gate%d_sb" % r) for r in range(2)]
-        warm = keep.tile([P, 2], F32, name="warm")
         ident = keep.tile([P, P], F32, name="ident")
         y_sb = keep.tile([P, S], F32, name="y_sb")
 
@@ -98,8 +97,6 @@ def tile_moe_elr_gelu_kernel(
                 )
 
         nc.vector.memset(xs_tok[:].bitcast(I32), 0)
-        nc.vector.memset(warm[:, 0:1], 0.0)
-        nc.scalar.activation(warm[:, 1:2], warm[:, 0:1], GELU)
 
         zeros = keep.tile([P, P], F32, name="ws_sb", align_bytes=256)
         nc.gpsimd.memset(zeros[:], 0.0)
@@ -114,8 +111,6 @@ def tile_moe_elr_gelu_kernel(
         )
         ws_sb = keep.tile([P, E * PASSES, N], U8, name="ws_sb", align_bytes=256)
         for r in range(4):
-            load_scales(nc.gpsimd, ws_sb[:, 0:E, :], WB_ROW, wb_scales, r)
-        for r in range(4):
             load_scales(nc.gpsimd, ws_sb, 0, w_scales, r)
 
         nc.sync.dma_start(offs_sb[:], offs)
@@ -125,10 +120,16 @@ def tile_moe_elr_gelu_kernel(
             )
         nc.sync.dma_start(x_tok[:], x_words.rearrange("s p t d -> p s (t d)").bitcast(I32))
         load_wa(0, 1)
-        for g in range(3):
-            for q in range(4):
+        quarters = [(g, q) for g in range(E // 2) for q in range(4)]
+        for e, run in ((1, quarters[0:4]), (3, quarters[4:10])):
+            for g, q in run:
                 load_was(g, q)
-            load_wa(2 * g + 1, min(2 * g + 3, 6))
+            load_wa(e, e + 2)
+        for g, q in quarters[10:15]:
+            load_was(g, q)
+        load_wa(5, 6)
+        load_wa(6, 7)
+        load_was(*quarters[15])
 
         gather_bytes(0, 384)
         gather_bytes(384, 768)
@@ -138,20 +139,18 @@ def tile_moe_elr_gelu_kernel(
         for j in range(256, S, 256):
             gather_words(j, j + 256)
 
-        for a in range(2):
-            for q in (2 * a, 2 * a + 1):
-                load_was(3, q)
-            for r in (2 * a, 2 * a + 1):
-                move_scales(r)
-            if a == 0:
-                load_wa(6, 7)
+        for r in range(4):
+            move_scales(r)
         for a in range(2):
             load_wa(7, 8, hid=slice(a * H // 2, (a + 1) * H // 2))
-        for g in range(len(GROUPS) - 1):
-            load_wb(g)
-            load_w(g)
-        load_w(len(GROUPS) - 1)
-        load_wb(len(GROUPS) - 1)
+        load_wb(0)
+        load_w(0)
+        for r in range(4):
+            load_scales(nc.sync, ws_sb[:, 0:E, :], WB_ROW, wb_scales, r)
+        load_wb(1)
+        load_w(1)
+        load_w(2)
+        load_wb(2)
         for r in range(2):
             nc.sync.dma_start(pos_sb[r][:], (pos1, pos2)[r])
             nc.sync.dma_start(gate_sb[r][:], gate[r])
@@ -210,40 +209,40 @@ def tile_moe_elr_gelu_kernel(
                 grouped[e0 // 2][:, (e0 % 2) * 4 * C : (e0 % 2 + e1 - e0) * 4 * C],
             )
 
-        def second_layer(order, pool, tag, evacuate):
-            first = min(order)
-            y = pool.tile([P, 4, P], F32, name=tag)
-            for e in order:
-                g = [k for k, (e0, e1) in enumerate(GROUPS) if e0 <= e < e1][0]
-                at = e - GROUPS[g][0]
-                cols = slice(e * C, (e + 1) * C)
-                acc = y[:, e - first, :]
-                passes = [
-                    (wb_sb[g][:, at, :].bitcast(FP8X4), ws_sb[WB_ROW:P, e, :], h_codes[:, cols], h_scales[:, cols])
-                ]
-                for s in range(PASSES):
-                    passes.append(
-                        (
-                            w_sb[g][:, PASSES * at + s, :].bitcast(FP4X4),
-                            ws_sb[:, PASSES * e + s, :],
-                            x_slot[s][:, cols],
-                            xs_slot[s][:, cols],
-                        )
-                    )
-                if e == E - 1:
-                    passes = passes[1:] + passes[:1]
-                for k, (weights, weight_scales, words, scales) in enumerate(passes):
-                    nc.tensor.matmul_mx(
-                        acc,
-                        lhsT=weights,
-                        lhsT_scale=weight_scales,
-                        rhs=words.bitcast(FP8X4),
-                        rhs_scale=scales,
-                        start=(k == 0),
-                        stop=(k == len(passes) - 1),
-                    )
-            n = len(order)
-            evacuate(y_sb[:, first * C : (first + n) * C], y[:, 0:n, :].rearrange("p e j -> p (e j)"))
+        def adapter_pass(acc, e, start, stop):
+            g = e // 3
+            cols = slice(e * C, (e + 1) * C)
+            nc.tensor.matmul_mx(
+                acc,
+                lhsT=wb_sb[g][:, e - GROUPS[g][0], :].bitcast(FP8X4),
+                lhsT_scale=ws_sb[WB_ROW:P, e, :],
+                rhs=h_codes[:, cols].bitcast(FP8X4),
+                rhs_scale=h_scales[:, cols],
+                start=start,
+                stop=stop,
+            )
+
+        def frozen_passes(acc, e, start, stop):
+            g = e // 3
+            cols = slice(e * C, (e + 1) * C)
+            for s in range(PASSES):
+                nc.tensor.matmul_mx(
+                    acc,
+                    lhsT=w_sb[g][:, PASSES * (e - GROUPS[g][0]) + s, :].bitcast(FP4X4),
+                    lhsT_scale=ws_sb[:, PASSES * e + s, :],
+                    rhs=x_slot[s][:, cols].bitcast(FP8X4),
+                    rhs_scale=xs_slot[s][:, cols],
+                    start=(start and s == 0),
+                    stop=(stop and s == PASSES - 1),
+                )
+
+        def second_layer(g):
+            e0, e1 = GROUPS[g]
+            y = psum.tile([P, 4, C], F32, name="spare%d" % g)
+            for e in range(e0, e1):
+                adapter_pass(y[:, e - e0, :], e, True, False)
+                frozen_passes(y[:, e - e0, :], e, False, True)
+            nc.vector.tensor_copy(y_sb[:, e0 * C : e1 * C], y[:, 0 : e1 - e0, :].rearrange("p e j -> p (e j)"))
 
         for e in range(E - 1):
             first_layer(e)
@@ -252,25 +251,29 @@ def tile_moe_elr_gelu_kernel(
                 turn(e - 2, banks[e][1])
             activate(e, 1)
             if e >= 2:
-                regroup(e - 2, nc.scalar.copy if e < 6 else nc.vector.tensor_copy)
+                regroup(e - 2, nc.vector.tensor_copy)
             if e in (3, 5):
                 quantise(e - 3, e - 1)
         turn(5, banks[6][0])
         regroup(5, nc.vector.tensor_copy)
         quantise(4, 6)
-        turn(6, psum.tile([P, H], F32, name="spare1"))
-        regroup(6, nc.scalar.copy)
-        quantise(6, 7)
         first_layer(7)
         activate(7, 0)
+        turn(6, psum.tile([P, H], F32, name="spare1"))
         activate(7, 1)
-        second_layer((0, 1), psum, "spare0", nc.vector.tensor_copy)
+        regroup(6, nc.vector.tensor_copy)
+        quantise(6, 7)
         turn(7, banks[7][1])
         regroup(7, nc.scalar.copy)
         quantise(7, 8)
-        second_layer((2, 3, 4), psum, "spare1", nc.vector.tensor_copy)
-        second_layer((5, 6), psum, "spare0", nc.vector.tensor_copy)
-        second_layer((7,), psum_h, "bank0", nc.scalar.copy)
+        second_layer(0)
+        second_layer(1)
+        last = [psum_h.tile([P, H], F32, name="bank%d" % a) for a in range(2)]
+        for a in range(2):
+            frozen_passes(last[a][:, 0:C], 6 + a, True, False)
+        for a, evacuate in enumerate((nc.vector.tensor_copy, nc.scalar.copy)):
+            adapter_pass(last[a][:, 0:C], 6 + a, False, True)
+            evacuate(y_sb[:, (6 + a) * C : (7 + a) * C], last[a][:, 0:C])
 
         half = T // 2
         prod = [keep.tile([P, T], F32, name="prod%d" % r) for r in range(2)]

@@ -5,7 +5,9 @@ import concourse.mybir as mybir
 K, T, E, C, H, N = 1024, 512, 8, 128, 512, 128
 S = E * C
 P = 128
-PASSES = 2
+PASSES = K // 512
+QUADRANTS = 4
+LAST = E - 1
 
 F32 = mybir.dt.float32
 BF16 = mybir.dt.bfloat16
@@ -21,73 +23,66 @@ ADD = mybir.AluOpType.add
 
 FLOPS = 2 * S * (K * H + K * N + H * N)
 
+ALIGN = 256
 X_ROW = (0, 4)
 WB_ROW = 8
-GROUPS = ((0, 3), (3, 6), (6, 8))
+W_GROUP = 3
+BYTE_GATHER = 384
+LAG = 2
+HALF_H = H // 2
+HALF_T = T // 2
 
 
 def tile_moe_elr_gelu_kernel(
     tc, x_words, x_scales, w_words, w_scales, wa_words, wa_scales, wb_words, wb_scales, gate, offs, pos1, pos2, out
 ):
     nc = tc.nc
+    w_groups = [(e, min(e + W_GROUP, E)) for e in range(0, E, W_GROUP)]
     with ExitStack() as ctx:
         keep = ctx.enter_context(tc.tile_pool(name="keep", bufs=1))
-        ring = ctx.enter_context(tc.tile_pool(name="ring", bufs=4))
-        psum_h = ctx.enter_context(tc.psum_pool(name="psum_h", bufs=3))
+        ring = ctx.enter_context(tc.tile_pool(name="ring", bufs=LAG + 2))
+        psum_h = ctx.enter_context(tc.psum_pool(name="psum_h", bufs=LAG + 1))
         psum = ctx.enter_context(tc.psum_pool(name="psum", bufs=1))
 
         offs_sb = keep.tile([P, S // 16], U16, name="offs_sb")
         pos_sb = [keep.tile([P, T // 16], U16, name="pos%d_sb" % r) for r in range(2)]
-        x_tok = keep.tile([P, PASSES, T], I32, name="x_tok", align_bytes=256)
-        xs_tok = keep.tile([P, T], U8, name="xs_tok", align_bytes=256)
-        x_slot = [keep.tile([P, S], I32, name="x_slot%d" % s, align_bytes=256) for s in range(PASSES)]
-        xs_slot = [keep.tile([P, S], U8, name="xs_slot%d" % s, align_bytes=256) for s in range(PASSES)]
-        wa_sb = keep.tile([P, E * PASSES, H], I32, name="wa_sb", align_bytes=256)
-        was_sb = keep.tile([P, E // 2, H], U8, name="was_sb", align_bytes=256)
+        x_tok = keep.tile([P, PASSES, T], I32, name="x_tok", align_bytes=ALIGN)
+        xs_tok = keep.tile([P, T], U8, name="xs_tok", align_bytes=ALIGN)
+        x_slot = [keep.tile([P, S], I32, name="x_slot%d" % s, align_bytes=ALIGN) for s in range(PASSES)]
+        xs_slot = [keep.tile([P, S], U8, name="xs_slot%d" % s, align_bytes=ALIGN) for s in range(PASSES)]
+        wa_sb = keep.tile([P, E * PASSES, H], I32, name="wa_sb", align_bytes=ALIGN)
+        was_sb = keep.tile([P, E // 2, H], U8, name="was_sb", align_bytes=ALIGN)
         w_sb = [
-            keep.tile([P, (e1 - e0) * PASSES, 2 * N], U8, name="w_sb%d" % e0, align_bytes=256) for e0, e1 in GROUPS
+            keep.tile([P, (e1 - e0) * PASSES, 2 * N], U8, name="w_sb%d" % e0, align_bytes=ALIGN) for e0, e1 in w_groups
         ]
-        wb_sb = [keep.tile([P, e1 - e0, N], I32, name="wb_sb%d" % e0, align_bytes=256) for e0, e1 in GROUPS]
+        wb_sb = keep.tile([P, E, N], I32, name="wb_sb", align_bytes=ALIGN)
+        wbs_sb = keep.tile([P, E, N], U8, name="wbs_sb", align_bytes=ALIGN)
         gate_sb = [keep.tile([P, T], F32, name="gate%d_sb" % r) for r in range(2)]
         ident = keep.tile([P, P], F32, name="ident")
         y_sb = keep.tile([P, S], F32, name="y_sb")
 
-        def load_was(g, q):
+        def load_wa(e0, e1):
             nc.sync.dma_start(
-                was_sb[32 * q : 32 * q + 16, g, :].bitcast(I32),
-                wa_scales[2 * g : 2 * g + 2, :, 4 * q : 4 * q + 4, :].rearrange("e s r i -> (e s) r i").bitcast(I32),
+                wa_sb[:, PASSES * e0 : PASSES * e1, :],
+                wa_words.rearrange("e s p i d -> p (e s) (i d)").bitcast(I32)[:, PASSES * e0 : PASSES * e1, :],
             )
 
-        def load_wa(e0, e1, hid=slice(0, H)):
-            nc.sync.dma_start(
-                wa_sb[:, PASSES * e0 : PASSES * e1, hid],
-                wa_words.rearrange("e s p i d -> p (e s) (i d)").bitcast(I32)[:, PASSES * e0 : PASSES * e1, hid],
-            )
+        def load_wa_scales(first, last):
+            for piece in range(first, last):
+                g, q = divmod(piece, QUADRANTS)
+                nc.sync.dma_start(
+                    was_sb[32 * q : 32 * q + 16, g, :].bitcast(I32),
+                    wa_scales[2 * g : 2 * g + 2, :, 4 * q : 4 * q + 4, :]
+                    .rearrange("e s r i -> (e s) r i")
+                    .bitcast(I32),
+                )
 
-        def load_wb(g):
-            e0, e1 = GROUPS[g]
-            nc.sync.dma_start(
-                wb_sb[g][:], wb_words.rearrange("e o p n d -> p (e o) (n d)").bitcast(I32)[:, e0:e1, :]
-            )
-
-        def load_w(g):
-            e0, e1 = GROUPS[g]
-            nc.sync.dma_start(
-                w_sb[g][:].bitcast(I32),
-                w_words.rearrange("e s p b -> p (e s) b").bitcast(I32)[:, PASSES * e0 : PASSES * e1, :],
-            )
-
-        def load_scales(queue, plane, first_row, scales, r):
-            queue.dma_start(
-                plane[first_row + r : P : 32, :, :].bitcast(I32),
-                scales.rearrange("e s (q r) n -> r q (e s) n", r=4)[r].bitcast(I32),
-            )
-
-        def move_scales(r):
-            nc.sync.dma_start(xs_slot[1][r:P:32, :].bitcast(I32), xs_slot[0][4 + r : P : 32, :].bitcast(I32))
-
-        def gather_bytes(j0, j1):
-            nc.vector.tensor_copy(xs_slot[0][:, j0:j1], xs_tok[:].indirect(offs_sb[:, j0 // 16 : j1 // 16]))
+        def load_planes(queue, planes, first_row, scales):
+            for r in range(4):
+                queue.dma_start(
+                    planes[first_row + r : P : 32, :, :].bitcast(I32),
+                    scales.rearrange("e s (q r) n -> r q (e s) n", r=4)[r].bitcast(I32),
+                )
 
         def gather_words(j0, j1):
             for s in range(PASSES):
@@ -96,9 +91,9 @@ def tile_moe_elr_gelu_kernel(
                     x_tok[:, s, :].bitcast(U32).indirect(offs_sb[:, j0 // 16 : j1 // 16]),
                 )
 
-        nc.vector.memset(xs_tok[:].bitcast(I32), 0)
+        nc.gpsimd.memset(xs_tok[:].bitcast(I32), 0)
 
-        zeros = keep.tile([P, P], F32, name="ws_sb", align_bytes=256)
+        zeros = keep.tile([P, P], F32, name="ws_sb", align_bytes=ALIGN)
         nc.gpsimd.memset(zeros[:], 0.0)
         nc.gpsimd.affine_select(
             out=ident[:],
@@ -109,69 +104,64 @@ def tile_moe_elr_gelu_kernel(
             pattern=[[-1, P]],
             channel_multiplier=1,
         )
-        ws_sb = keep.tile([P, E * PASSES, N], U8, name="ws_sb", align_bytes=256)
-        for r in range(4):
-            load_scales(nc.gpsimd, ws_sb, 0, w_scales, r)
+        ws_sb = keep.tile([P, E * PASSES, N], U8, name="ws_sb", align_bytes=ALIGN)
+        load_planes(nc.gpsimd, ws_sb, 0, w_scales)
 
         nc.sync.dma_start(offs_sb[:], offs)
-        for q in range(4):
+        for q in range(QUADRANTS):
             nc.sync.dma_start(
                 xs_tok[32 * q : 32 * q + 8, :].bitcast(I32), x_scales[:, 4 * q : 4 * q + 4, :].bitcast(I32)
             )
         nc.sync.dma_start(x_tok[:], x_words.rearrange("s p t d -> p s (t d)").bitcast(I32))
         load_wa(0, 1)
-        quarters = [(g, q) for g in range(E // 2) for q in range(4)]
-        for e, run in ((1, quarters[0:4]), (3, quarters[4:10])):
-            for g, q in run:
-                load_was(g, q)
-            load_wa(e, e + 2)
-        for g, q in quarters[10:15]:
-            load_was(g, q)
+        load_wa_scales(0, 4)
+        load_wa(1, 3)
+        load_wa_scales(4, 10)
+        load_wa(3, 5)
+        load_wa_scales(10, 15)
         load_wa(5, 6)
         load_wa(6, 7)
-        load_was(*quarters[15])
+        load_wa_scales(15, 16)
+        load_planes(nc.sync, wbs_sb, WB_ROW, wb_scales)
+        load_wa(LAST, E)
+        nc.sync.dma_start(wb_sb[:], wb_words.rearrange("e o p n d -> p (e o) (n d)").bitcast(I32))
 
-        gather_bytes(0, 384)
-        gather_bytes(384, 768)
-        gather_bytes(768, S)
-        gather_words(0, 128)
-        gather_words(128, 256)
-        for j in range(256, S, 256):
-            gather_words(j, j + 256)
+        for j in range(0, S, BYTE_GATHER):
+            j1 = min(j + BYTE_GATHER, S)
+            nc.vector.tensor_copy(xs_slot[0][:, j:j1], xs_tok[:].indirect(offs_sb[:, j // 16 : j1 // 16]))
+        gather_words(0, C)
+        gather_words(C, 2 * C)
+        for j in range(2 * C, S, 2 * C):
+            gather_words(j, j + 2 * C)
 
         for r in range(4):
-            move_scales(r)
-        for a in range(2):
-            load_wa(7, 8, hid=slice(a * H // 2, (a + 1) * H // 2))
-        load_wb(0)
-        load_w(0)
-        for r in range(4):
-            load_scales(nc.sync, ws_sb[:, 0:E, :], WB_ROW, wb_scales, r)
-        load_wb(1)
-        load_w(1)
-        load_w(2)
-        load_wb(2)
-        for r in range(2):
-            nc.sync.dma_start(pos_sb[r][:], (pos1, pos2)[r])
+            nc.sync.dma_start(
+                xs_slot[1][r:P:32, :].bitcast(I32), xs_slot[0][X_ROW[1] + r : P : 32, :].bitcast(I32)
+            )
+        for g, (e0, e1) in enumerate(w_groups):
+            nc.sync.dma_start(
+                w_sb[g][:].bitcast(I32),
+                w_words.rearrange("e s p b -> p (e s) b").bitcast(I32)[:, PASSES * e0 : PASSES * e1, :],
+            )
+        for r, pos in enumerate((pos1, pos2)):
+            nc.sync.dma_start(pos_sb[r][:], pos)
             nc.sync.dma_start(gate_sb[r][:], gate[r])
 
-        h_words = {}
-        grouped = [keep.tile([P, 2 * 4 * C], BF16, name="grouped%d" % a, align_bytes=256) for a in range(E // 2)]
-        h_codes = keep.tile([P, S], U32, name="h_codes", align_bytes=256)
-        h_scales = keep.tile([P, S], U8, name="h_scales", align_bytes=256)
-
+        grouped = [keep.tile([P, 2 * 4 * C], BF16, name="grouped%d" % a, align_bytes=ALIGN) for a in range(E // 2)]
+        h_codes = keep.tile([P, S], U32, name="h_codes", align_bytes=ALIGN)
+        h_scales = keep.tile([P, S], U8, name="h_scales", align_bytes=ALIGN)
         banks = {}
+        h_rows = {}
         turned = {}
-        half_h = H // 2
 
-        def first_layer(e):
+        def first_product(e):
             cols = slice(e * C, (e + 1) * C)
             banks[e] = [psum_h.tile([P, H], F32, name="bank%d" % a) for a in range(2)]
             for a in range(2):
-                hid = slice(a * half_h, (a + 1) * half_h)
+                hid = slice(a * HALF_H, (a + 1) * HALF_H)
                 for s in range(PASSES):
                     nc.tensor.matmul_mx(
-                        banks[e][a][:, 0:half_h],
+                        banks[e][a][:, 0:HALF_H],
                         lhsT=x_slot[s][:, cols].bitcast(FP8X4),
                         lhsT_scale=xs_slot[0][X_ROW[s] : P, cols],
                         rhs=wa_sb[:, PASSES * e + s, hid].bitcast(FP8X4),
@@ -182,16 +172,16 @@ def tile_moe_elr_gelu_kernel(
 
         def activate(e, a):
             if a == 0:
-                h_words[e] = ring.tile([P, H], BF16, name="h", align_bytes=256)
+                h_rows[e] = ring.tile([P, H], BF16, name="h", align_bytes=ALIGN)
             nc.scalar.activation(
-                h_words[e][:].rearrange("j (u p b) -> j u p b", u=2, b=2)[:, :, 64 * a : 64 * (a + 1), :],
-                banks[e][a][:, 0:half_h].rearrange("j (p u b) -> j u p b", u=2, b=2),
+                h_rows[e][:].rearrange("j (u p b) -> j u p b", u=2, b=2)[:, :, P // 2 * a : P // 2 * (a + 1), :],
+                banks[e][a][:, 0:HALF_H].rearrange("j (p u b) -> j u p b", u=2, b=2),
                 GELU,
             )
 
         def turn(e, bank):
-            words = h_words[e][:].bitcast(F32)
-            turned[e] = bank[:, half_h:H].rearrange("p (u j) -> p u j", u=2)
+            words = h_rows[e][:].bitcast(F32)
+            turned[e] = bank[:, HALF_H:H].rearrange("p (u j) -> p u j", u=2)
             for u in range(2):
                 nc.tensor.transpose(turned[e][:, u, :], words[:, u * P : (u + 1) * P], ident[:])
 
@@ -209,85 +199,75 @@ def tile_moe_elr_gelu_kernel(
                 grouped[e0 // 2][:, (e0 % 2) * 4 * C : (e0 % 2 + e1 - e0) * 4 * C],
             )
 
-        def adapter_pass(acc, e, start, stop):
-            g = e // 3
+        def adapter_pass(acc, e, opens):
             cols = slice(e * C, (e + 1) * C)
             nc.tensor.matmul_mx(
                 acc,
-                lhsT=wb_sb[g][:, e - GROUPS[g][0], :].bitcast(FP8X4),
-                lhsT_scale=ws_sb[WB_ROW:P, e, :],
+                lhsT=wb_sb[:, e, :].bitcast(FP8X4),
+                lhsT_scale=wbs_sb[WB_ROW:P, e, :],
                 rhs=h_codes[:, cols].bitcast(FP8X4),
                 rhs_scale=h_scales[:, cols],
-                start=start,
-                stop=stop,
+                start=opens,
+                stop=not opens,
             )
 
-        def frozen_passes(acc, e, start, stop):
-            g = e // 3
+        def frozen_passes(acc, e, opens):
             cols = slice(e * C, (e + 1) * C)
             for s in range(PASSES):
                 nc.tensor.matmul_mx(
                     acc,
-                    lhsT=w_sb[g][:, PASSES * (e - GROUPS[g][0]) + s, :].bitcast(FP4X4),
+                    lhsT=w_sb[e // W_GROUP][:, PASSES * (e % W_GROUP) + s, :].bitcast(FP4X4),
                     lhsT_scale=ws_sb[:, PASSES * e + s, :],
                     rhs=x_slot[s][:, cols].bitcast(FP8X4),
                     rhs_scale=xs_slot[s][:, cols],
-                    start=(start and s == 0),
-                    stop=(stop and s == PASSES - 1),
+                    start=(opens and s == 0),
+                    stop=(not opens and s == PASSES - 1),
                 )
 
-        def second_layer(g):
-            e0, e1 = GROUPS[g]
-            y = psum.tile([P, 4, C], F32, name="spare%d" % g)
-            for e in range(e0, e1):
-                adapter_pass(y[:, e - e0, :], e, True, False)
-                frozen_passes(y[:, e - e0, :], e, False, True)
-            nc.vector.tensor_copy(y_sb[:, e0 * C : e1 * C], y[:, 0 : e1 - e0, :].rearrange("p e j -> p (e j)"))
-
-        for e in range(E - 1):
-            first_layer(e)
+        for e in range(LAST):
+            first_product(e)
             activate(e, 0)
-            if e >= 2:
-                turn(e - 2, banks[e][1])
+            if e >= LAG:
+                turn(e - LAG, banks[e][1])
             activate(e, 1)
-            if e >= 2:
-                regroup(e - 2, nc.vector.tensor_copy)
-            if e in (3, 5):
-                quantise(e - 3, e - 1)
-        turn(5, banks[6][0])
-        regroup(5, nc.vector.tensor_copy)
-        quantise(4, 6)
-        first_layer(7)
-        activate(7, 0)
-        turn(6, psum.tile([P, H], F32, name="spare1"))
-        activate(7, 1)
-        regroup(6, nc.vector.tensor_copy)
-        quantise(6, 7)
-        turn(7, banks[7][1])
-        regroup(7, nc.scalar.copy)
-        quantise(7, 8)
-        second_layer(0)
-        second_layer(1)
-        last = [psum_h.tile([P, H], F32, name="bank%d" % a) for a in range(2)]
-        for a in range(2):
-            frozen_passes(last[a][:, 0:C], 6 + a, True, False)
-        for a, evacuate in enumerate((nc.vector.tensor_copy, nc.scalar.copy)):
-            adapter_pass(last[a][:, 0:C], 6 + a, False, True)
-            evacuate(y_sb[:, (6 + a) * C : (7 + a) * C], last[a][:, 0:C])
+            if e >= LAG:
+                regroup(e - LAG, nc.vector.tensor_copy)
+                if (e - LAG) % 2 == 1:
+                    quantise(e - LAG - 1, e - LAG + 1)
 
-        half = T // 2
+        turn(LAST - 2, banks[LAST - 1][0])
+        regroup(LAST - 2, nc.vector.tensor_copy)
+        quantise(LAST - 3, LAST - 1)
+        first_product(LAST)
+        activate(LAST, 0)
+        turn(LAST - 1, psum.tile([P, H], F32, name="spare1"))
+        activate(LAST, 1)
+        regroup(LAST - 1, nc.vector.tensor_copy)
+        quantise(LAST - 1, LAST)
+        turn(LAST, banks[LAST][1])
+        regroup(LAST, nc.scalar.copy)
+        quantise(LAST, E)
+
+        sums = [psum.tile([P, H], F32, name="spare0")]
+        sums.extend(psum_h.tile([P, H], F32, name="bank%d" % (k % 2)) for k in range(2 * LAG))
+        sums.append(psum.tile([P, H], F32, name="spare1"))
+        sums.extend(psum_h.tile([P, H], F32, name="bank%d" % a) for a in range(2))
+        for e in range(LAST):
+            adapter_pass(sums[e][:, 0:C], e, True)
+        for e in range(E):
+            frozen_passes(sums[e][:, 0:C], e, e == LAST)
+            if e == LAST:
+                adapter_pass(sums[e][:, 0:C], e, False)
+            evacuate = nc.scalar.copy if e % 2 else nc.vector.tensor_copy
+            evacuate(y_sb[:, e * C : (e + 1) * C], sums[e][:, 0:C])
+
         prod = [keep.tile([P, T], F32, name="prod%d" % r) for r in range(2)]
-        res = [keep.tile([P, half], F32, name="res%d" % a) for a in range(2)]
-
-        def combine(r, t0, t1):
+        res = [keep.tile([P, HALF_T], F32, name="res%d" % a) for a in range(2)]
+        for r, t0, t1 in ((0, 0, T), (1, 0, HALF_T), (1, HALF_T, T)):
             nc.vector.tensor_tensor(
                 prod[r][:, t0:t1], y_sb[:].indirect(pos_sb[r][:, t0 // 16 : t1 // 16]), gate_sb[r][:, t0:t1], MULT
             )
-
-        combine(0, 0, T)
-        combine(1, 0, half)
-        combine(1, half, T)
         for a in range(2):
-            cols = slice(a * half, (a + 1) * half)
+            cols = slice(a * HALF_T, (a + 1) * HALF_T)
             nc.vector.tensor_tensor(res[a][:], prod[0][:, cols], prod[1][:, cols], ADD)
             nc.sync.dma_start(out[:, cols], res[a][:])

@@ -25,12 +25,13 @@ FLOPS = 2 * S * (K * H + K * N + H * N)
 
 ALIGN = 256
 X_ROW = (0, 4)
+EARLY = 2
+LATE_ROW = 12
 WB_ROW = 8
 W_GROUP = 3
-BYTE_GATHER = 384
+SCALAR_REGROUPS = 2
 LAG = 2
 HALF_H = H // 2
-HALF_T = T // 2
 
 
 def tile_moe_elr_gelu_kernel(
@@ -50,8 +51,8 @@ def tile_moe_elr_gelu_kernel(
         xs_tok = keep.tile([P, T], U8, name="xs_tok", align_bytes=ALIGN)
         x_slot = [keep.tile([P, S], I32, name="x_slot%d" % s, align_bytes=ALIGN) for s in range(PASSES)]
         xs_slot = [keep.tile([P, S], U8, name="xs_slot%d" % s, align_bytes=ALIGN) for s in range(PASSES)]
-        wa_sb = keep.tile([P, E * PASSES, H], I32, name="wa_sb", align_bytes=ALIGN)
-        was_sb = keep.tile([P, E // 2, H], U8, name="was_sb", align_bytes=ALIGN)
+        wa_sb = {}
+        was_sb = keep.tile([P, EARLY // 2, H], U8, name="was_sb", align_bytes=ALIGN)
         w_sb = [
             keep.tile([P, (e1 - e0) * PASSES, 2 * N], U8, name="w_sb%d" % e0, align_bytes=ALIGN) for e0, e1 in w_groups
         ]
@@ -62,10 +63,12 @@ def tile_moe_elr_gelu_kernel(
         y_sb = keep.tile([P, S], F32, name="y_sb")
 
         def load_wa(e0, e1):
+            group = keep.tile([P, (e1 - e0) * PASSES, H], I32, name="wa_sb%d" % e0, align_bytes=ALIGN)
             nc.sync.dma_start(
-                wa_sb[:, PASSES * e0 : PASSES * e1, :],
-                wa_words.rearrange("e s p i d -> p (e s) (i d)").bitcast(I32)[:, PASSES * e0 : PASSES * e1, :],
+                group[:], wa_words.rearrange("e s p i d -> p (e s) (i d)").bitcast(I32)[:, PASSES * e0 : PASSES * e1, :]
             )
+            for e in range(e0, e1):
+                wa_sb[e] = group[:, PASSES * (e - e0) : PASSES * (e - e0 + 1), :]
 
         def load_wa_scales(first, last):
             for piece in range(first, last):
@@ -91,9 +94,12 @@ def tile_moe_elr_gelu_kernel(
                     x_tok[:, s, :].bitcast(U32).indirect(offs_sb[:, j0 // 16 : j1 // 16]),
                 )
 
-        nc.gpsimd.memset(xs_tok[:].bitcast(I32), 0)
+        def gather_bytes(j0, j1):
+            nc.vector.tensor_copy(xs_slot[0][:, j0:j1], xs_tok[:].indirect(offs_sb[:, j0 // 16 : j1 // 16]))
 
-        zeros = keep.tile([P, P], F32, name="ws_sb", align_bytes=ALIGN)
+        nc.vector.memset(xs_tok[:].bitcast(I32), 0)
+
+        zeros = keep.tile([P, P], F32, name="was_late", align_bytes=ALIGN)
         nc.gpsimd.memset(zeros[:], 0.0)
         nc.gpsimd.affine_select(
             out=ident[:],
@@ -104,35 +110,30 @@ def tile_moe_elr_gelu_kernel(
             pattern=[[-1, P]],
             channel_multiplier=1,
         )
-        ws_sb = keep.tile([P, E * PASSES, N], U8, name="ws_sb", align_bytes=ALIGN)
-        load_planes(nc.gpsimd, ws_sb, 0, w_scales)
+        was_late = keep.tile([P, (E - EARLY) * PASSES, H], U8, name="was_late", align_bytes=ALIGN)
+        load_planes(nc.gpsimd, was_late, LATE_ROW, wa_scales[EARLY:E])
 
-        nc.sync.dma_start(offs_sb[:], offs)
+        nc.sync.dma_start(x_tok[:], x_words.rearrange("s p t d -> p s (t d)").bitcast(I32))
         for q in range(QUADRANTS):
             nc.sync.dma_start(
                 xs_tok[32 * q : 32 * q + 8, :].bitcast(I32), x_scales[:, 4 * q : 4 * q + 4, :].bitcast(I32)
             )
-        nc.sync.dma_start(x_tok[:], x_words.rearrange("s p t d -> p s (t d)").bitcast(I32))
+        nc.sync.dma_start(offs_sb[:], offs)
         load_wa(0, 1)
         load_wa_scales(0, 4)
-        load_wa(1, 3)
-        load_wa_scales(4, 10)
-        load_wa(3, 5)
-        load_wa_scales(10, 15)
-        load_wa(5, 6)
-        load_wa(6, 7)
-        load_wa_scales(15, 16)
+        for e in range(1, E):
+            load_wa(e, e + 1)
         load_planes(nc.sync, wbs_sb, WB_ROW, wb_scales)
-        load_wa(LAST, E)
         nc.sync.dma_start(wb_sb[:], wb_words.rearrange("e o p n d -> p (e o) (n d)").bitcast(I32))
 
-        for j in range(0, S, BYTE_GATHER):
-            j1 = min(j + BYTE_GATHER, S)
-            nc.vector.tensor_copy(xs_slot[0][:, j:j1], xs_tok[:].indirect(offs_sb[:, j // 16 : j1 // 16]))
+        gather_bytes(0, 2 * C)
         gather_words(0, C)
         gather_words(C, 2 * C)
-        for j in range(2 * C, S, 2 * C):
-            gather_words(j, j + 2 * C)
+        gather_bytes(2 * C, 5 * C)
+        gather_words(2 * C, 4 * C)
+        gather_bytes(5 * C, S)
+        gather_words(4 * C, 6 * C)
+        gather_words(6 * C, S)
 
         for r in range(4):
             nc.sync.dma_start(
@@ -164,8 +165,12 @@ def tile_moe_elr_gelu_kernel(
                         banks[e][a][:, 0:HALF_H],
                         lhsT=x_slot[s][:, cols].bitcast(FP8X4),
                         lhsT_scale=xs_slot[0][X_ROW[s] : P, cols],
-                        rhs=wa_sb[:, PASSES * e + s, hid].bitcast(FP8X4),
-                        rhs_scale=was_sb[4 * (PASSES * (e % 2) + s) : P, e // 2, hid],
+                        rhs=wa_sb[e][:, s, hid].bitcast(FP8X4),
+                        rhs_scale=(
+                            was_sb[4 * (PASSES * (e % 2) + s) : P, e // 2, hid]
+                            if e < EARLY
+                            else was_late[LATE_ROW:P, PASSES * (e - EARLY) + s, hid]
+                        ),
                         start=(s == 0),
                         stop=(s == PASSES - 1),
                     )
@@ -226,12 +231,15 @@ def tile_moe_elr_gelu_kernel(
 
         for e in range(LAST):
             first_product(e)
+            if e == 0:
+                ws_sb = keep.tile([P, E * PASSES, N], U8, name="wa_sb0", align_bytes=ALIGN)
+                load_planes(nc.gpsimd, ws_sb, 0, w_scales)
             activate(e, 0)
             if e >= LAG:
                 turn(e - LAG, banks[e][1])
             activate(e, 1)
             if e >= LAG:
-                regroup(e - LAG, nc.vector.tensor_copy)
+                regroup(e - LAG, nc.scalar.copy if e - LAG < SCALAR_REGROUPS else nc.vector.tensor_copy)
                 if (e - LAG) % 2 == 1:
                     quantise(e - LAG - 1, e - LAG + 1)
 
@@ -262,12 +270,24 @@ def tile_moe_elr_gelu_kernel(
             evacuate(y_sb[:, e * C : (e + 1) * C], sums[e][:, 0:C])
 
         prod = [keep.tile([P, T], F32, name="prod%d" % r) for r in range(2)]
-        res = [keep.tile([P, HALF_T], F32, name="res%d" % a) for a in range(2)]
-        for r, t0, t1 in ((0, 0, T), (1, 0, HALF_T), (1, HALF_T, T)):
+        pieces = [slice(0, T // 2), slice(T // 2, 3 * T // 4), slice(3 * T // 4, T)]
+        res = [keep.tile([P, c.stop - c.start], F32, name="res%d" % a) for a, c in enumerate(pieces)]
+
+        def fetch(r, cols):
             nc.vector.tensor_tensor(
-                prod[r][:, t0:t1], y_sb[:].indirect(pos_sb[r][:, t0 // 16 : t1 // 16]), gate_sb[r][:, t0:t1], MULT
+                prod[r][:, cols],
+                y_sb[:].indirect(pos_sb[r][:, cols.start // 16 : cols.stop // 16]),
+                gate_sb[r][:, cols],
+                MULT,
             )
-        for a in range(2):
-            cols = slice(a * HALF_T, (a + 1) * HALF_T)
-            nc.vector.tensor_tensor(res[a][:], prod[0][:, cols], prod[1][:, cols], ADD)
-            nc.sync.dma_start(out[:, cols], res[a][:])
+
+        def finish(a):
+            nc.vector.tensor_tensor(res[a][:], prod[0][:, pieces[a]], prod[1][:, pieces[a]], ADD)
+            nc.sync.dma_start(out[:, pieces[a]], res[a][:])
+
+        fetch(0, slice(0, T))
+        for a, cols in enumerate(pieces):
+            fetch(1, cols)
+            if a > 0:
+                finish(a - 1)
+        finish(len(pieces) - 1)

@@ -234,21 +234,21 @@ def tile_moe_elr_gelu_kernel(
             if e == 0:
                 ws_sb = keep.tile([P, E * PASSES, N], U8, name="wa_sb0", align_bytes=ALIGN)
                 load_planes(nc.gpsimd, ws_sb, 0, w_scales)
-            activate(e, 0)
-            if e >= LAG:
-                turn(e - LAG, banks[e][1])
-            activate(e, 1)
-            if e >= LAG:
-                regroup(e - LAG, nc.scalar.copy if e - LAG < SCALAR_REGROUPS else nc.vector.tensor_copy)
-                if (e - LAG) % 2 == 1:
-                    quantise(e - LAG - 1, e - LAG + 1)
+            if e >= 2 and e % 2 == 0:
+                activate(e, 0)
+                turn(e - 2, banks[e][1])
+                turn(e - 1, banks[e][0])
+                activate(e, 1)
+                for d in (e - 2, e - 1):
+                    regroup(d, nc.scalar.copy if d < SCALAR_REGROUPS else nc.vector.tensor_copy)
+                quantise(e - 2, e)
+            else:
+                activate(e, 0)
+                activate(e, 1)
 
-        turn(LAST - 2, banks[LAST - 1][0])
-        regroup(LAST - 2, nc.vector.tensor_copy)
-        quantise(LAST - 3, LAST - 1)
         first_product(LAST)
         activate(LAST, 0)
-        turn(LAST - 1, psum.tile([P, H], F32, name="spare1"))
+        turn(LAST - 1, banks[LAST][0])
         activate(LAST, 1)
         regroup(LAST - 1, nc.vector.tensor_copy)
         quantise(LAST - 1, LAST)
@@ -256,15 +256,13 @@ def tile_moe_elr_gelu_kernel(
         regroup(LAST, nc.scalar.copy)
         quantise(LAST, E)
 
-        sums = [psum.tile([P, H], F32, name="spare0")]
-        sums.extend(psum_h.tile([P, H], F32, name="bank%d" % (k % 2)) for k in range(2 * LAG))
-        sums.append(psum.tile([P, H], F32, name="spare1"))
-        sums.extend(psum_h.tile([P, H], F32, name="bank%d" % a) for a in range(2))
-        for e in range(LAST):
+        sums = [psum.tile([P, H], F32, name="spare%d" % k) for k in range(2)]
+        sums.extend(psum_h.tile([P, H], F32, name="bank%d" % (k % 2)) for k in range(E - 2))
+        for e in range(LAST - 1):
             adapter_pass(sums[e][:, 0:C], e, True)
         for e in range(E):
-            frozen_passes(sums[e][:, 0:C], e, e == LAST)
-            if e == LAST:
+            frozen_passes(sums[e][:, 0:C], e, e >= LAST - 1)
+            if e >= LAST - 1:
                 adapter_pass(sums[e][:, 0:C], e, False)
             evacuate = nc.scalar.copy if e % 2 else nc.vector.tensor_copy
             evacuate(y_sb[:, e * C : (e + 1) * C], sums[e][:, 0:C])

@@ -25,12 +25,11 @@ FLOPS = 2 * S * (K * H + K * N + H * N)
 
 ALIGN = 256
 X_ROW = (0, 4)
-EARLY = 2
-LATE_ROW = 12
 WB_ROW = 8
-W_GROUP = 3
+W_GROUP = 4
 SCALAR_REGROUPS = 2
 LAG = 2
+RUN = 6
 HALF_H = H // 2
 
 
@@ -52,12 +51,11 @@ def tile_moe_elr_gelu_kernel(
         x_slot = [keep.tile([P, S], I32, name="x_slot%d" % s, align_bytes=ALIGN) for s in range(PASSES)]
         xs_slot = [keep.tile([P, S], U8, name="xs_slot%d" % s, align_bytes=ALIGN) for s in range(PASSES)]
         wa_sb = {}
-        was_sb = keep.tile([P, EARLY // 2, H], U8, name="was_sb", align_bytes=ALIGN)
+        was_sb = keep.tile([P, E // 2, H], U8, name="was_sb", align_bytes=ALIGN)
         w_sb = [
             keep.tile([P, (e1 - e0) * PASSES, 2 * N], U8, name="w_sb%d" % e0, align_bytes=ALIGN) for e0, e1 in w_groups
         ]
         wb_sb = keep.tile([P, E, N], I32, name="wb_sb", align_bytes=ALIGN)
-        wbs_sb = keep.tile([P, E, N], U8, name="wbs_sb", align_bytes=ALIGN)
         gate_sb = [keep.tile([P, T], F32, name="gate%d_sb" % r) for r in range(2)]
         ident = keep.tile([P, P], F32, name="ident")
         y_sb = keep.tile([P, S], F32, name="y_sb")
@@ -99,7 +97,7 @@ def tile_moe_elr_gelu_kernel(
 
         nc.vector.memset(xs_tok[:].bitcast(I32), 0)
 
-        zeros = keep.tile([P, P], F32, name="was_late", align_bytes=ALIGN)
+        zeros = keep.tile([P, P], F32, name="ws_sb", align_bytes=ALIGN)
         nc.gpsimd.memset(zeros[:], 0.0)
         nc.gpsimd.affine_select(
             out=ident[:],
@@ -110,8 +108,11 @@ def tile_moe_elr_gelu_kernel(
             pattern=[[-1, P]],
             channel_multiplier=1,
         )
-        was_late = keep.tile([P, (E - EARLY) * PASSES, H], U8, name="was_late", align_bytes=ALIGN)
-        load_planes(nc.gpsimd, was_late, LATE_ROW, wa_scales[EARLY:E])
+        planes = keep.tile([P, E * (PASSES + 1), N], U8, name="ws_sb", align_bytes=ALIGN)
+        ws_sb = planes[:, 0 : E * PASSES, :]
+        wbs_sb = planes[:, E * PASSES :, :]
+        load_planes(nc.gpsimd, ws_sb, 0, w_scales)
+        load_planes(nc.gpsimd, wbs_sb, WB_ROW, wb_scales)
 
         nc.sync.dma_start(x_tok[:], x_words.rearrange("s p t d -> p s (t d)").bitcast(I32))
         for q in range(QUADRANTS):
@@ -119,12 +120,12 @@ def tile_moe_elr_gelu_kernel(
                 xs_tok[32 * q : 32 * q + 8, :].bitcast(I32), x_scales[:, 4 * q : 4 * q + 4, :].bitcast(I32)
             )
         nc.sync.dma_start(offs_sb[:], offs)
-        load_wa(0, 1)
-        load_wa_scales(0, 4)
-        for e in range(1, E):
-            load_wa(e, e + 1)
-        load_planes(nc.sync, wbs_sb, WB_ROW, wb_scales)
-        nc.sync.dma_start(wb_sb[:], wb_words.rearrange("e o p n d -> p (e o) (n d)").bitcast(I32))
+        pieces = E // 2 * QUADRANTS
+        for g in range(E // 2 - 1):
+            load_wa(2 * g, 2 * g + 2)
+            load_wa_scales(RUN * g, min(RUN * (g + 1), pieces))
+        load_wa(LAST - 1, LAST)
+        load_wa(LAST, E)
 
         gather_bytes(0, 2 * C)
         gather_words(0, C)
@@ -135,14 +136,19 @@ def tile_moe_elr_gelu_kernel(
         gather_words(4 * C, 6 * C)
         gather_words(6 * C, S)
 
-        for r in range(4):
-            nc.sync.dma_start(
-                xs_slot[1][r:P:32, :].bitcast(I32), xs_slot[0][X_ROW[1] + r : P : 32, :].bitcast(I32)
-            )
         for g, (e0, e1) in enumerate(w_groups):
             nc.sync.dma_start(
                 w_sb[g][:].bitcast(I32),
                 w_words.rearrange("e s p b -> p (e s) b").bitcast(I32)[:, PASSES * e0 : PASSES * e1, :],
+            )
+            if g == 0:
+                for r in range(4):
+                    nc.sync.dma_start(
+                        xs_slot[1][r:P:32, :].bitcast(I32), xs_slot[0][X_ROW[1] + r : P : 32, :].bitcast(I32)
+                    )
+        for half in (slice(0, E // 2), slice(E // 2, E)):
+            nc.sync.dma_start(
+                wb_sb[:, half, :], wb_words.rearrange("e o p n d -> p (e o) (n d)").bitcast(I32)[:, half, :]
             )
         for r, pos in enumerate((pos1, pos2)):
             nc.sync.dma_start(pos_sb[r][:], pos)
@@ -166,11 +172,7 @@ def tile_moe_elr_gelu_kernel(
                         lhsT=x_slot[s][:, cols].bitcast(FP8X4),
                         lhsT_scale=xs_slot[0][X_ROW[s] : P, cols],
                         rhs=wa_sb[e][:, s, hid].bitcast(FP8X4),
-                        rhs_scale=(
-                            was_sb[4 * (PASSES * (e % 2) + s) : P, e // 2, hid]
-                            if e < EARLY
-                            else was_late[LATE_ROW:P, PASSES * (e - EARLY) + s, hid]
-                        ),
+                        rhs_scale=was_sb[4 * (PASSES * (e % 2) + s) : P, e // 2, hid],
                         start=(s == 0),
                         stop=(s == PASSES - 1),
                     )
@@ -216,24 +218,20 @@ def tile_moe_elr_gelu_kernel(
                 stop=not opens,
             )
 
-        def frozen_passes(acc, e, opens):
+        def frozen_pass(acc, e, s):
             cols = slice(e * C, (e + 1) * C)
-            for s in range(PASSES):
-                nc.tensor.matmul_mx(
-                    acc,
-                    lhsT=w_sb[e // W_GROUP][:, PASSES * (e % W_GROUP) + s, :].bitcast(FP4X4),
-                    lhsT_scale=ws_sb[:, PASSES * e + s, :],
-                    rhs=x_slot[s][:, cols].bitcast(FP8X4),
-                    rhs_scale=xs_slot[s][:, cols],
-                    start=(opens and s == 0),
-                    stop=(not opens and s == PASSES - 1),
-                )
+            nc.tensor.matmul_mx(
+                acc,
+                lhsT=w_sb[e // W_GROUP][:, PASSES * (e % W_GROUP) + s, :].bitcast(FP4X4),
+                lhsT_scale=ws_sb[:, PASSES * e + s, :],
+                rhs=x_slot[s][:, cols].bitcast(FP8X4),
+                rhs_scale=xs_slot[s][:, cols],
+                start=(s == 0),
+                stop=False,
+            )
 
         for e in range(LAST):
             first_product(e)
-            if e == 0:
-                ws_sb = keep.tile([P, E * PASSES, N], U8, name="wa_sb0", align_bytes=ALIGN)
-                load_planes(nc.gpsimd, ws_sb, 0, w_scales)
             if e >= 2 and e % 2 == 0:
                 activate(e, 0)
                 turn(e - 2, banks[e][1])
@@ -258,12 +256,11 @@ def tile_moe_elr_gelu_kernel(
 
         sums = [psum.tile([P, H], F32, name="spare%d" % k) for k in range(2)]
         sums.extend(psum_h.tile([P, H], F32, name="bank%d" % (k % 2)) for k in range(E - 2))
-        for e in range(LAST - 1):
-            adapter_pass(sums[e][:, 0:C], e, True)
         for e in range(E):
-            frozen_passes(sums[e][:, 0:C], e, e >= LAST - 1)
-            if e >= LAST - 1:
-                adapter_pass(sums[e][:, 0:C], e, False)
+            for s in range(PASSES):
+                frozen_pass(sums[e][:, 0:C], e, s)
+        for e in range(E):
+            adapter_pass(sums[e][:, 0:C], e, False)
             evacuate = nc.scalar.copy if e % 2 else nc.vector.tensor_copy
             evacuate(y_sb[:, e * C : (e + 1) * C], sums[e][:, 0:C])
 

@@ -25,8 +25,10 @@ FLOPS = 2 * S * (K * H + K * N + H * N)
 
 ALIGN = 256
 X_ROW = (0, 4)
+EARLY = 4
+LATE_ROW = 12
 WB_ROW = 8
-W_GROUP = 4
+W_GROUP = 8
 SCALAR_REGROUPS = 2
 LAG = 2
 RUN = 6
@@ -51,7 +53,7 @@ def tile_moe_elr_gelu_kernel(
         x_slot = [keep.tile([P, S], I32, name="x_slot%d" % s, align_bytes=ALIGN) for s in range(PASSES)]
         xs_slot = [keep.tile([P, S], U8, name="xs_slot%d" % s, align_bytes=ALIGN) for s in range(PASSES)]
         wa_sb = {}
-        was_sb = keep.tile([P, E // 2, H], U8, name="was_sb", align_bytes=ALIGN)
+        was_sb = keep.tile([P, EARLY // 2, H], U8, name="was_sb", align_bytes=ALIGN)
         w_sb = [
             keep.tile([P, (e1 - e0) * PASSES, 2 * N], U8, name="w_sb%d" % e0, align_bytes=ALIGN) for e0, e1 in w_groups
         ]
@@ -78,8 +80,8 @@ def tile_moe_elr_gelu_kernel(
                     .bitcast(I32),
                 )
 
-        def load_planes(queue, planes, first_row, scales):
-            for r in range(4):
+        def load_planes(queue, planes, first_row, scales, rows):
+            for r in rows:
                 queue.dma_start(
                     planes[first_row + r : P : 32, :, :].bitcast(I32),
                     scales.rearrange("e s (q r) n -> r q (e s) n", r=4)[r].bitcast(I32),
@@ -97,7 +99,7 @@ def tile_moe_elr_gelu_kernel(
 
         nc.vector.memset(xs_tok[:].bitcast(I32), 0)
 
-        zeros = keep.tile([P, P], F32, name="ws_sb", align_bytes=ALIGN)
+        zeros = keep.tile([P, P], F32, name="was_late", align_bytes=ALIGN)
         nc.gpsimd.memset(zeros[:], 0.0)
         nc.gpsimd.affine_select(
             out=ident[:],
@@ -108,11 +110,9 @@ def tile_moe_elr_gelu_kernel(
             pattern=[[-1, P]],
             channel_multiplier=1,
         )
-        planes = keep.tile([P, E * (PASSES + 1), N], U8, name="ws_sb", align_bytes=ALIGN)
-        ws_sb = planes[:, 0 : E * PASSES, :]
-        wbs_sb = planes[:, E * PASSES :, :]
-        load_planes(nc.gpsimd, ws_sb, 0, w_scales)
-        load_planes(nc.gpsimd, wbs_sb, WB_ROW, wb_scales)
+        was_late = keep.tile([P, (E - EARLY) * PASSES, H], U8, name="was_late", align_bytes=ALIGN)
+        ws_sb = keep.tile([P, E * PASSES, N], U8, name="ws_sb", align_bytes=ALIGN)
+        load_planes(nc.gpsimd, was_late, LATE_ROW, wa_scales[EARLY:E], range(3))
 
         nc.sync.dma_start(x_tok[:], x_words.rearrange("s p t d -> p s (t d)").bitcast(I32))
         for q in range(QUADRANTS):
@@ -120,12 +120,14 @@ def tile_moe_elr_gelu_kernel(
                 xs_tok[32 * q : 32 * q + 8, :].bitcast(I32), x_scales[:, 4 * q : 4 * q + 4, :].bitcast(I32)
             )
         nc.sync.dma_start(offs_sb[:], offs)
-        pieces = E // 2 * QUADRANTS
-        for g in range(E // 2 - 1):
-            load_wa(2 * g, 2 * g + 2)
-            load_wa_scales(RUN * g, min(RUN * (g + 1), pieces))
-        load_wa(LAST - 1, LAST)
-        load_wa(LAST, E)
+        load_wa(0, 2)
+        load_wa_scales(0, RUN)
+        load_wa(2, 4)
+        load_wa_scales(RUN, EARLY // 2 * QUADRANTS)
+        load_planes(nc.sync, was_late, LATE_ROW, wa_scales[EARLY:E], range(3, 4))
+        for e in range(EARLY, E):
+            load_wa(e, e + 1)
+        load_planes(nc.sync, ws_sb, 0, w_scales, range(4))
 
         gather_bytes(0, 2 * C)
         gather_words(0, C)
@@ -172,7 +174,11 @@ def tile_moe_elr_gelu_kernel(
                         lhsT=x_slot[s][:, cols].bitcast(FP8X4),
                         lhsT_scale=xs_slot[0][X_ROW[s] : P, cols],
                         rhs=wa_sb[e][:, s, hid].bitcast(FP8X4),
-                        rhs_scale=was_sb[4 * (PASSES * (e % 2) + s) : P, e // 2, hid],
+                        rhs_scale=(
+                            was_sb[4 * (PASSES * (e % 2) + s) : P, e // 2, hid]
+                            if e < EARLY
+                            else was_late[LATE_ROW:P, PASSES * (e - EARLY) + s, hid]
+                        ),
                         start=(s == 0),
                         stop=(s == PASSES - 1),
                     )
@@ -232,6 +238,9 @@ def tile_moe_elr_gelu_kernel(
 
         for e in range(LAST):
             first_product(e)
+            if e == 1:
+                wbs_sb = keep.tile([P, E, N], U8, name="wa_sb0", align_bytes=ALIGN)
+                load_planes(nc.gpsimd, wbs_sb, WB_ROW, wb_scales, range(4))
             if e >= 2 and e % 2 == 0:
                 activate(e, 0)
                 turn(e - 2, banks[e][1])

@@ -33,6 +33,7 @@ SCALAR_REGROUPS = 2
 LAG = 2
 RUN = 6
 HALF_H = H // 2
+GROUPS = ((0, 2), (2, 4), (4, 5), (5, 7), (7, 8))
 
 
 def tile_moe_elr_gelu_kernel(
@@ -42,6 +43,7 @@ def tile_moe_elr_gelu_kernel(
     w_groups = [(e, min(e + W_GROUP, E)) for e in range(0, E, W_GROUP)]
     with ExitStack() as ctx:
         keep = ctx.enter_context(tc.tile_pool(name="keep", bufs=1))
+        late = ctx.enter_context(tc.tile_pool(name="late", bufs=1))
         ring = ctx.enter_context(tc.tile_pool(name="ring", bufs=LAG + 2))
         psum_h = ctx.enter_context(tc.psum_pool(name="psum_h", bufs=LAG + 1))
         psum = ctx.enter_context(tc.psum_pool(name="psum", bufs=1))
@@ -68,7 +70,20 @@ def tile_moe_elr_gelu_kernel(
                 group[:], wa_words.rearrange("e s p i d -> p (e s) (i d)").bitcast(I32)[:, PASSES * e0 : PASSES * e1, :]
             )
             for e in range(e0, e1):
-                wa_sb[e] = group[:, PASSES * (e - e0) : PASSES * (e - e0 + 1), :]
+                own = group[:, PASSES * (e - e0) : PASSES * (e - e0 + 1), :]
+                wa_sb[e] = [own[:, :, a * HALF_H : (a + 1) * HALF_H] for a in range(2)]
+
+        def load_wa_halves(e):
+            wa_sb[e] = []
+            for a in range(2):
+                half = keep.tile([P, PASSES, HALF_H], I32, name="wa_half%d" % a, align_bytes=ALIGN)
+                nc.sync.dma_start(
+                    half[:],
+                    wa_words.rearrange("e s p i d -> p (e s) (i d)").bitcast(I32)[
+                        :, PASSES * e : PASSES * (e + 1), a * HALF_H : (a + 1) * HALF_H
+                    ],
+                )
+                wa_sb[e].append(half[:])
 
         def load_wa_scales(first, last):
             for piece in range(first, last):
@@ -99,20 +114,27 @@ def tile_moe_elr_gelu_kernel(
 
         nc.vector.memset(xs_tok[:].bitcast(I32), 0)
 
-        zeros = keep.tile([P, P], F32, name="was_late", align_bytes=ALIGN)
-        nc.gpsimd.memset(zeros[:], 0.0)
+        late_bytes = (E - EARLY) * PASSES * H
+        ws_bytes = E * PASSES * N
+        wbs_bytes = E * N
+        cover = late.tile([P, (late_bytes + ws_bytes + wbs_bytes) // 4], F32, name="zeros", align_bytes=ALIGN, offset=0)
+        zeros = cover[:, 0:P]
+        nc.gpsimd.memset(zeros, 0.0)
         nc.gpsimd.affine_select(
             out=ident[:],
-            in_=zeros[:],
+            in_=zeros,
             compare_op=mybir.AluOpType.not_equal,
             fill=1.0,
             base=0,
             pattern=[[-1, P]],
             channel_multiplier=1,
         )
-        was_late = keep.tile([P, (E - EARLY) * PASSES, H], U8, name="was_late", align_bytes=ALIGN)
-        ws_sb = keep.tile([P, E * PASSES, N], U8, name="ws_sb", align_bytes=ALIGN)
+        was_late = late.tile([P, (E - EARLY) * PASSES, H], U8, name="was_late", align_bytes=ALIGN, offset=0)
+        ws_sb = late.tile([P, E * PASSES, N], U8, name="ws_sb", align_bytes=ALIGN, offset=late_bytes)
+        wbs_sb = late.tile([P, E, N], U8, name="wbs_sb", align_bytes=ALIGN, offset=late_bytes + ws_bytes)
         load_planes(nc.gpsimd, was_late, LATE_ROW, wa_scales[EARLY:E], range(3))
+        load_planes(nc.gpsimd, ws_sb, 0, w_scales, range(3))
+        load_planes(nc.gpsimd, wbs_sb, WB_ROW, wb_scales, range(4))
 
         nc.sync.dma_start(x_tok[:], x_words.rearrange("s p t d -> p s (t d)").bitcast(I32))
         for q in range(QUADRANTS):
@@ -125,9 +147,10 @@ def tile_moe_elr_gelu_kernel(
         load_wa(2, 4)
         load_wa_scales(RUN, EARLY // 2 * QUADRANTS)
         load_planes(nc.sync, was_late, LATE_ROW, wa_scales[EARLY:E], range(3, 4))
-        for e in range(EARLY, E):
+        for e in range(EARLY, LAST):
             load_wa(e, e + 1)
-        load_planes(nc.sync, ws_sb, 0, w_scales, range(4))
+        load_wa_halves(LAST)
+        load_planes(nc.sync, ws_sb, 0, w_scales, range(3, 4))
 
         gather_bytes(0, 2 * C)
         gather_words(0, C)
@@ -152,11 +175,17 @@ def tile_moe_elr_gelu_kernel(
             nc.sync.dma_start(
                 wb_sb[:, half, :], wb_words.rearrange("e o p n d -> p (e o) (n d)").bitcast(I32)[:, half, :]
             )
-        for r, pos in enumerate((pos1, pos2)):
-            nc.sync.dma_start(pos_sb[r][:], pos)
-            nc.sync.dma_start(gate_sb[r][:], gate[r])
+        halves = (slice(0, T // 2), slice(T // 2, T))
+        nc.sync.dma_start(pos_sb[0][:], pos1)
+        for cols in halves:
+            nc.sync.dma_start(gate_sb[0][:, cols], gate[0][:, cols])
+        nc.sync.dma_start(pos_sb[1][:], pos2)
+        nc.sync.dma_start(gate_sb[1][:], gate[1])
 
-        grouped = [keep.tile([P, 2 * 4 * C], BF16, name="grouped%d" % a, align_bytes=ALIGN) for a in range(E // 2)]
+        grouped = {
+            e0: keep.tile([P, (e1 - e0) * 4 * C], BF16, name="grouped%d" % e0, align_bytes=ALIGN) for e0, e1 in GROUPS
+        }
+        group_of = {e: e0 for e0, e1 in GROUPS for e in range(e0, e1)}
         h_codes = keep.tile([P, S], U32, name="h_codes", align_bytes=ALIGN)
         h_scales = keep.tile([P, S], U8, name="h_scales", align_bytes=ALIGN)
         banks = {}
@@ -173,7 +202,7 @@ def tile_moe_elr_gelu_kernel(
                         banks[e][a][:, 0:HALF_H],
                         lhsT=x_slot[s][:, cols].bitcast(FP8X4),
                         lhsT_scale=xs_slot[0][X_ROW[s] : P, cols],
-                        rhs=wa_sb[e][:, s, hid].bitcast(FP8X4),
+                        rhs=wa_sb[e][a][:, s, :].bitcast(FP8X4),
                         rhs_scale=(
                             was_sb[4 * (PASSES * (e % 2) + s) : P, e // 2, hid]
                             if e < EARLY
@@ -192,15 +221,15 @@ def tile_moe_elr_gelu_kernel(
                 GELU,
             )
 
-        def turn(e, bank):
+        def turn(e, bank, first=HALF_H):
             words = h_rows[e][:].bitcast(F32)
-            turned[e] = bank[:, HALF_H:H].rearrange("p (u j) -> p u j", u=2)
+            turned[e] = bank[:, first : first + HALF_H].rearrange("p (u j) -> p u j", u=2)
             for u in range(2):
                 nc.tensor.transpose(turned[e][:, u, :], words[:, u * P : (u + 1) * P], ident[:])
 
         def regroup(e, copy):
             copy(
-                grouped[e // 2][:].bitcast(F32).rearrange("p (e j u) -> p e j u", e=2, u=2)[:, e % 2],
+                grouped[group_of[e]][:].bitcast(F32).rearrange("p (e j u) -> p e j u", j=C, u=2)[:, e - group_of[e]],
                 turned[e].rearrange("p u j -> p j u"),
             )
 
@@ -209,7 +238,7 @@ def tile_moe_elr_gelu_kernel(
             nc.vector.quantize_mx(
                 h_codes[:, cols].bitcast(FP8X4),
                 h_scales[:, cols],
-                grouped[e0 // 2][:, (e0 % 2) * 4 * C : (e0 % 2 + e1 - e0) * 4 * C],
+                grouped[e0][:],
             )
 
         def adapter_pass(acc, e, opens):
@@ -238,10 +267,7 @@ def tile_moe_elr_gelu_kernel(
 
         for e in range(LAST):
             first_product(e)
-            if e == 1:
-                wbs_sb = keep.tile([P, E, N], U8, name="wa_sb0", align_bytes=ALIGN)
-                load_planes(nc.gpsimd, wbs_sb, WB_ROW, wb_scales, range(4))
-            if e >= 2 and e % 2 == 0:
+            if e in (2, 4):
                 activate(e, 0)
                 turn(e - 2, banks[e][1])
                 turn(e - 1, banks[e][0])
@@ -249,24 +275,34 @@ def tile_moe_elr_gelu_kernel(
                 for d in (e - 2, e - 1):
                     regroup(d, nc.scalar.copy if d < SCALAR_REGROUPS else nc.vector.tensor_copy)
                 quantise(e - 2, e)
+            elif e == 5:
+                activate(e, 0)
+                turn(e - 1, banks[e][0])
+                activate(e, 1)
+                regroup(e - 1, nc.vector.tensor_copy)
+                quantise(e - 1, e)
             else:
                 activate(e, 0)
                 activate(e, 1)
 
         first_product(LAST)
         activate(LAST, 0)
+        turn(LAST - 2, banks[LAST][0], 0)
         turn(LAST - 1, banks[LAST][0])
         activate(LAST, 1)
-        regroup(LAST - 1, nc.vector.tensor_copy)
-        quantise(LAST - 1, LAST)
+        nc.vector.tensor_copy(
+            grouped[LAST - 2][:].bitcast(F32).rearrange("p (e j u) -> p e j u", j=C, u=2),
+            banks[LAST][0][:].rearrange("p (e u j) -> p e j u", e=2, u=2),
+        )
+        quantise(LAST - 2, LAST)
         turn(LAST, banks[LAST][1])
         regroup(LAST, nc.scalar.copy)
         quantise(LAST, E)
 
         sums = [psum.tile([P, H], F32, name="spare%d" % k) for k in range(2)]
         sums.extend(psum_h.tile([P, H], F32, name="bank%d" % (k % 2)) for k in range(E - 2))
-        for e in range(E):
-            for s in range(PASSES):
+        for s in range(PASSES):
+            for e in range(E):
                 frozen_pass(sums[e][:, 0:C], e, s)
         for e in range(E):
             adapter_pass(sums[e][:, 0:C], e, False)
@@ -289,7 +325,8 @@ def tile_moe_elr_gelu_kernel(
             nc.vector.tensor_tensor(res[a][:], prod[0][:, pieces[a]], prod[1][:, pieces[a]], ADD)
             nc.sync.dma_start(out[:, pieces[a]], res[a][:])
 
-        fetch(0, slice(0, T))
+        for cols in halves:
+            fetch(0, cols)
         for a, cols in enumerate(pieces):
             fetch(1, cols)
             if a > 0:

@@ -31,7 +31,6 @@ WB_ROW = 8
 W_GROUP = 8
 SCALAR_REGROUPS = 2
 LAG = 2
-RUN = 6
 HALF_H = H // 2
 GROUPS = ((0, 2), (2, 4), (4, 5), (5, 7), (7, 8))
 
@@ -43,7 +42,6 @@ def tile_moe_elr_gelu_kernel(
     w_groups = [(e, min(e + W_GROUP, E)) for e in range(0, E, W_GROUP)]
     with ExitStack() as ctx:
         keep = ctx.enter_context(tc.tile_pool(name="keep", bufs=1))
-        late = ctx.enter_context(tc.tile_pool(name="late", bufs=1))
         ring = ctx.enter_context(tc.tile_pool(name="ring", bufs=LAG + 2))
         psum_h = ctx.enter_context(tc.psum_pool(name="psum_h", bufs=LAG + 1))
         psum = ctx.enter_context(tc.psum_pool(name="psum", bufs=1))
@@ -64,26 +62,15 @@ def tile_moe_elr_gelu_kernel(
         ident = keep.tile([P, P], F32, name="ident")
         y_sb = keep.tile([P, S], F32, name="y_sb")
 
-        def load_wa(e0, e1):
-            group = keep.tile([P, (e1 - e0) * PASSES, H], I32, name="wa_sb%d" % e0, align_bytes=ALIGN)
+        def load_wa(first, last, cols=slice(0, H)):
+            width = cols.stop - cols.start
+            group = keep.tile([P, last - first, width], I32, name="wa_sb%d_%d" % (first, cols.start), align_bytes=ALIGN)
             nc.sync.dma_start(
-                group[:], wa_words.rearrange("e s p i d -> p (e s) (i d)").bitcast(I32)[:, PASSES * e0 : PASSES * e1, :]
+                group[:], wa_words.rearrange("e s p i d -> p (e s) (i d)").bitcast(I32)[:, first:last, cols]
             )
-            for e in range(e0, e1):
-                own = group[:, PASSES * (e - e0) : PASSES * (e - e0 + 1), :]
-                wa_sb[e] = [own[:, :, a * HALF_H : (a + 1) * HALF_H] for a in range(2)]
-
-        def load_wa_halves(e):
-            wa_sb[e] = []
-            for a in range(2):
-                half = keep.tile([P, PASSES, HALF_H], I32, name="wa_half%d" % a, align_bytes=ALIGN)
-                nc.sync.dma_start(
-                    half[:],
-                    wa_words.rearrange("e s p i d -> p (e s) (i d)").bitcast(I32)[
-                        :, PASSES * e : PASSES * (e + 1), a * HALF_H : (a + 1) * HALF_H
-                    ],
-                )
-                wa_sb[e].append(half[:])
+            for m in range(first, last):
+                for a in range(cols.start // HALF_H, cols.stop // HALF_H):
+                    wa_sb[m, a] = group[:, m - first, a * HALF_H - cols.start : (a + 1) * HALF_H - cols.start]
 
         def load_wa_scales(first, last):
             for piece in range(first, last):
@@ -114,27 +101,20 @@ def tile_moe_elr_gelu_kernel(
 
         nc.vector.memset(xs_tok[:].bitcast(I32), 0)
 
-        late_bytes = (E - EARLY) * PASSES * H
-        ws_bytes = E * PASSES * N
-        wbs_bytes = E * N
-        cover = late.tile([P, (late_bytes + ws_bytes + wbs_bytes) // 4], F32, name="zeros", align_bytes=ALIGN, offset=0)
-        zeros = cover[:, 0:P]
-        nc.gpsimd.memset(zeros, 0.0)
+        zeros = keep.tile([P, P], F32, name="was_late", align_bytes=ALIGN)
+        nc.gpsimd.memset(zeros[:], 0.0)
         nc.gpsimd.affine_select(
             out=ident[:],
-            in_=zeros,
+            in_=zeros[:],
             compare_op=mybir.AluOpType.not_equal,
             fill=1.0,
             base=0,
             pattern=[[-1, P]],
             channel_multiplier=1,
         )
-        was_late = late.tile([P, (E - EARLY) * PASSES, H], U8, name="was_late", align_bytes=ALIGN, offset=0)
-        ws_sb = late.tile([P, E * PASSES, N], U8, name="ws_sb", align_bytes=ALIGN, offset=late_bytes)
-        wbs_sb = late.tile([P, E, N], U8, name="wbs_sb", align_bytes=ALIGN, offset=late_bytes + ws_bytes)
+        was_late = keep.tile([P, (E - EARLY) * PASSES, H], U8, name="was_late", align_bytes=ALIGN)
+        ws_sb = keep.tile([P, E * PASSES, N], U8, name="ws_sb", align_bytes=ALIGN)
         load_planes(nc.gpsimd, was_late, LATE_ROW, wa_scales[EARLY:E], range(3))
-        load_planes(nc.gpsimd, ws_sb, 0, w_scales, range(3))
-        load_planes(nc.gpsimd, wbs_sb, WB_ROW, wb_scales, range(4))
 
         nc.sync.dma_start(x_tok[:], x_words.rearrange("s p t d -> p s (t d)").bitcast(I32))
         for q in range(QUADRANTS):
@@ -142,24 +122,22 @@ def tile_moe_elr_gelu_kernel(
                 xs_tok[32 * q : 32 * q + 8, :].bitcast(I32), x_scales[:, 4 * q : 4 * q + 4, :].bitcast(I32)
             )
         nc.sync.dma_start(offs_sb[:], offs)
-        load_wa(0, 2)
-        load_wa_scales(0, RUN)
-        load_wa(2, 4)
-        load_wa_scales(RUN, EARLY // 2 * QUADRANTS)
+        load_wa(0, 3)
+        load_wa_scales(0, QUADRANTS)
+        load_wa(3, 6)
+        load_wa_scales(QUADRANTS, 2 * QUADRANTS)
+        load_wa(6, 8)
         load_planes(nc.sync, was_late, LATE_ROW, wa_scales[EARLY:E], range(3, 4))
         for e in range(EARLY, LAST):
-            load_wa(e, e + 1)
-        load_wa_halves(LAST)
-        load_planes(nc.sync, ws_sb, 0, w_scales, range(3, 4))
+            load_wa(PASSES * e, PASSES * (e + 1))
+        for a in range(2):
+            load_wa(PASSES * LAST, PASSES * E, slice(a * HALF_H, (a + 1) * HALF_H))
+        load_planes(nc.sync, ws_sb, 0, w_scales, range(4))
 
-        gather_bytes(0, 2 * C)
-        gather_words(0, C)
-        gather_words(C, 2 * C)
-        gather_bytes(2 * C, 5 * C)
-        gather_words(2 * C, 4 * C)
-        gather_bytes(5 * C, S)
-        gather_words(4 * C, 6 * C)
-        gather_words(6 * C, S)
+        for e in range(E):
+            if e % 2 == 0:
+                gather_bytes(e * C, (e + 2) * C)
+            gather_words(e * C, (e + 1) * C)
 
         for g, (e0, e1) in enumerate(w_groups):
             nc.sync.dma_start(
@@ -202,7 +180,7 @@ def tile_moe_elr_gelu_kernel(
                         banks[e][a][:, 0:HALF_H],
                         lhsT=x_slot[s][:, cols].bitcast(FP8X4),
                         lhsT_scale=xs_slot[0][X_ROW[s] : P, cols],
-                        rhs=wa_sb[e][a][:, s, :].bitcast(FP8X4),
+                        rhs=wa_sb[PASSES * e + s, a].bitcast(FP8X4),
                         rhs_scale=(
                             was_sb[4 * (PASSES * (e % 2) + s) : P, e // 2, hid]
                             if e < EARLY
@@ -267,6 +245,9 @@ def tile_moe_elr_gelu_kernel(
 
         for e in range(LAST):
             first_product(e)
+            if e == 1:
+                wbs_sb = keep.tile([P, E, N], U8, name="wa_sb0_0", align_bytes=ALIGN)
+                load_planes(nc.gpsimd, wbs_sb, WB_ROW, wb_scales, range(4))
             if e in (2, 4):
                 activate(e, 0)
                 turn(e - 2, banks[e][1])
@@ -277,7 +258,7 @@ def tile_moe_elr_gelu_kernel(
                 quantise(e - 2, e)
             elif e == 5:
                 activate(e, 0)
-                turn(e - 1, banks[e][0])
+                turn(e - 1, banks[e][1])
                 activate(e, 1)
                 regroup(e - 1, nc.vector.tensor_copy)
                 quantise(e - 1, e)
@@ -301,9 +282,10 @@ def tile_moe_elr_gelu_kernel(
 
         sums = [psum.tile([P, H], F32, name="spare%d" % k) for k in range(2)]
         sums.extend(psum_h.tile([P, H], F32, name="bank%d" % (k % 2)) for k in range(E - 2))
-        for s in range(PASSES):
-            for e in range(E):
-                frozen_pass(sums[e][:, 0:C], e, s)
+        for experts in (range(LAST - 1), range(LAST - 1, E)):
+            for s in range(PASSES):
+                for e in experts:
+                    frozen_pass(sums[e][:, 0:C], e, s)
         for e in range(E):
             adapter_pass(sums[e][:, 0:C], e, False)
             evacuate = nc.scalar.copy if e % 2 else nc.vector.tensor_copy

@@ -28,7 +28,7 @@ X_ROW = (0, 4)
 EARLY = 4
 LATE_ROW = 12
 WB_ROW = 8
-W_GROUP = 8
+W_GROUP = 4
 SCALAR_REGROUPS = 2
 LAG = 2
 HALF_H = H // 2
@@ -42,6 +42,7 @@ def tile_moe_elr_gelu_kernel(
     w_groups = [(e, min(e + W_GROUP, E)) for e in range(0, E, W_GROUP)]
     with ExitStack() as ctx:
         keep = ctx.enter_context(tc.tile_pool(name="keep", bufs=1))
+        late = ctx.enter_context(tc.tile_pool(name="late", bufs=1))
         ring = ctx.enter_context(tc.tile_pool(name="ring", bufs=LAG + 2))
         psum_h = ctx.enter_context(tc.psum_pool(name="psum_h", bufs=LAG + 1))
         psum = ctx.enter_context(tc.psum_pool(name="psum", bufs=1))
@@ -101,7 +102,8 @@ def tile_moe_elr_gelu_kernel(
 
         nc.vector.memset(xs_tok[:].bitcast(I32), 0)
 
-        zeros = keep.tile([P, P], F32, name="was_late", align_bytes=ALIGN)
+        late_bytes = (E - EARLY) * PASSES * H
+        zeros = late.tile([P, P], F32, name="zeros", align_bytes=ALIGN, offset=late_bytes - ALIGN)
         nc.gpsimd.memset(zeros[:], 0.0)
         nc.gpsimd.affine_select(
             out=ident[:],
@@ -112,9 +114,10 @@ def tile_moe_elr_gelu_kernel(
             pattern=[[-1, P]],
             channel_multiplier=1,
         )
-        was_late = keep.tile([P, (E - EARLY) * PASSES, H], U8, name="was_late", align_bytes=ALIGN)
-        ws_sb = keep.tile([P, E * PASSES, N], U8, name="ws_sb", align_bytes=ALIGN)
+        was_late = late.tile([P, (E - EARLY) * PASSES, H], U8, name="was_late", align_bytes=ALIGN, offset=0)
+        ws_sb = late.tile([P, E * PASSES, N], U8, name="ws_sb", align_bytes=ALIGN, offset=late_bytes)
         load_planes(nc.gpsimd, was_late, LATE_ROW, wa_scales[EARLY:E], range(3))
+        load_planes(nc.gpsimd, ws_sb, 0, w_scales, range(2))
 
         nc.sync.dma_start(x_tok[:], x_words.rearrange("s p t d -> p s (t d)").bitcast(I32))
         for q in range(QUADRANTS):
@@ -128,23 +131,23 @@ def tile_moe_elr_gelu_kernel(
         load_wa_scales(QUADRANTS, 2 * QUADRANTS)
         load_wa(6, 8)
         load_planes(nc.sync, was_late, LATE_ROW, wa_scales[EARLY:E], range(3, 4))
-        for e in range(EARLY, LAST):
+        for e in range(EARLY, E):
             load_wa(PASSES * e, PASSES * (e + 1))
-        for a in range(2):
-            load_wa(PASSES * LAST, PASSES * E, slice(a * HALF_H, (a + 1) * HALF_H))
-        load_planes(nc.sync, ws_sb, 0, w_scales, range(4))
+        load_planes(nc.sync, ws_sb, 0, w_scales, range(2, 4))
 
-        for e in range(E):
-            if e % 2 == 0:
-                gather_bytes(e * C, (e + 2) * C)
-            gather_words(e * C, (e + 1) * C)
+        gather_bytes(0, 2 * C)
+        gather_words(0, C)
+        gather_words(C, 2 * C)
+        for e in range(2, E, 2):
+            gather_bytes(e * C, (e + 2) * C)
+            gather_words(e * C, (e + 2) * C)
 
         for g, (e0, e1) in enumerate(w_groups):
             nc.sync.dma_start(
                 w_sb[g][:].bitcast(I32),
                 w_words.rearrange("e s p b -> p (e s) b").bitcast(I32)[:, PASSES * e0 : PASSES * e1, :],
             )
-            if g == 0:
+            if g == 1:
                 for r in range(4):
                     nc.sync.dma_start(
                         xs_slot[1][r:P:32, :].bitcast(I32), xs_slot[0][X_ROW[1] + r : P : 32, :].bitcast(I32)
@@ -282,10 +285,9 @@ def tile_moe_elr_gelu_kernel(
 
         sums = [psum.tile([P, H], F32, name="spare%d" % k) for k in range(2)]
         sums.extend(psum_h.tile([P, H], F32, name="bank%d" % (k % 2)) for k in range(E - 2))
-        for experts in (range(LAST - 1), range(LAST - 1, E)):
-            for s in range(PASSES):
-                for e in experts:
-                    frozen_pass(sums[e][:, 0:C], e, s)
+        for s in range(PASSES):
+            for e in range(E):
+                frozen_pass(sums[e][:, 0:C], e, s)
         for e in range(E):
             adapter_pass(sums[e][:, 0:C], e, False)
             evacuate = nc.scalar.copy if e % 2 else nc.vector.tensor_copy

@@ -18,6 +18,7 @@ U8 = mybir.dt.uint8
 FP8X4 = mybir.dt.float8_e4m3fn_x4
 FP4X4 = mybir.dt.float4_e2m1fn_x4
 GELU = mybir.ActivationFunctionType.Gelu_apprx_tanh
+COPY = mybir.ActivationFunctionType.Copy
 MULT = mybir.AluOpType.mult
 ADD = mybir.AluOpType.add
 
@@ -59,7 +60,7 @@ def tile_moe_elr_gelu_kernel(
             keep.tile([P, (e1 - e0) * PASSES, 2 * N], U8, name="w_sb%d" % e0, align_bytes=ALIGN) for e0, e1 in w_groups
         ]
         wb_sb = keep.tile([P, E, N], I32, name="wb_sb", align_bytes=ALIGN)
-        gate_sb = [keep.tile([P, T], F32, name="gate%d_sb" % r) for r in range(2)]
+        gate_sb = [keep.tile([P, 2, T // 2], F32, name="gate_sb%d" % g) for g in range(2)]
         ident = keep.tile([P, P], F32, name="ident")
         y_sb = keep.tile([P, S], F32, name="y_sb")
 
@@ -156,12 +157,10 @@ def tile_moe_elr_gelu_kernel(
             nc.sync.dma_start(
                 wb_sb[:, half, :], wb_words.rearrange("e o p n d -> p (e o) (n d)").bitcast(I32)[:, half, :]
             )
-        halves = (slice(0, T // 2), slice(T // 2, T))
-        nc.sync.dma_start(pos_sb[0][:], pos1)
-        for cols in halves:
-            nc.sync.dma_start(gate_sb[0][:, cols], gate[0][:, cols])
         nc.sync.dma_start(pos_sb[1][:], pos2)
-        nc.sync.dma_start(gate_sb[1][:], gate[1])
+        nc.sync.dma_start(pos_sb[0][:], pos1)
+        for g in range(2):
+            nc.sync.dma_start(gate_sb[g][:], gate.rearrange("r p t -> p r t")[:, :, g * T // 2 : (g + 1) * T // 2])
 
         grouped = {
             e0: keep.tile([P, (e1 - e0) * 4 * C], BF16, name="grouped%d" % e0, align_bytes=ALIGN) for e0, e1 in GROUPS
@@ -293,26 +292,20 @@ def tile_moe_elr_gelu_kernel(
             evacuate = nc.scalar.copy if e % 2 else nc.vector.tensor_copy
             evacuate(y_sb[:, e * C : (e + 1) * C], sums[e][:, 0:C])
 
+        picked = keep.tile([P, T], F32, name="picked")
         prod = [keep.tile([P, T], F32, name="prod%d" % r) for r in range(2)]
-        pieces = [slice(0, T // 2), slice(T // 2, 3 * T // 4), slice(3 * T // 4, T)]
+        halves = (slice(0, T // 2), slice(T // 2, T))
+        pieces = (halves[0], slice(T // 2, 3 * T // 4), slice(3 * T // 4, T))
         res = [keep.tile([P, c.stop - c.start], F32, name="res%d" % a) for a, c in enumerate(pieces)]
 
-        def fetch(r, cols):
-            nc.vector.tensor_tensor(
-                prod[r][:, cols],
-                y_sb[:].indirect(pos_sb[r][:, cols.start // 16 : cols.stop // 16]),
-                gate_sb[r][:, cols],
-                MULT,
-            )
+        def listed(r, cols):
+            return y_sb[:].indirect(pos_sb[r][:, cols.start // 16 : cols.stop // 16])
 
-        def finish(a):
-            nc.vector.tensor_tensor(res[a][:], prod[0][:, pieces[a]], prod[1][:, pieces[a]], ADD)
-            nc.sync.dma_start(out[:, pieces[a]], res[a][:])
-
-        for cols in halves:
-            fetch(0, cols)
+        for g, cols in enumerate(halves):
+            nc.scalar.activation(picked[:, cols], listed(1, cols), COPY)
+            nc.vector.tensor_tensor(prod[0][:, cols], listed(0, cols), gate_sb[g][:, 0, :], MULT)
+        for g, cols in enumerate(halves):
+            nc.vector.tensor_tensor(prod[1][:, cols], picked[:, cols], gate_sb[g][:, 1, :], MULT)
         for a, cols in enumerate(pieces):
-            fetch(1, cols)
-            if a > 0:
-                finish(a - 1)
-        finish(len(pieces) - 1)
+            nc.vector.tensor_tensor(res[a][:], prod[0][:, cols], prod[1][:, cols], ADD)
+            nc.sync.dma_start(out[:, cols], res[a][:])

@@ -60,7 +60,7 @@ def tile_moe_elr_gelu_kernel(
             keep.tile([P, (e1 - e0) * PASSES, 2 * N], U8, name="w_sb%d" % e0, align_bytes=ALIGN) for e0, e1 in w_groups
         ]
         wb_sb = keep.tile([P, E, N], I32, name="wb_sb", align_bytes=ALIGN)
-        gate_sb = [keep.tile([P, 2, T // 2], F32, name="gate_sb%d" % g) for g in range(2)]
+        gate_sb = [keep.tile([P, T], F32, name="gate_sb%d" % r) for r in range(2)]
         ident = keep.tile([P, P], F32, name="ident")
         y_sb = keep.tile([P, S], F32, name="y_sb")
 
@@ -159,8 +159,10 @@ def tile_moe_elr_gelu_kernel(
             )
         nc.sync.dma_start(pos_sb[1][:], pos2)
         nc.sync.dma_start(pos_sb[0][:], pos1)
-        for g in range(2):
-            nc.sync.dma_start(gate_sb[g][:], gate.rearrange("r p t -> p r t")[:, :, g * T // 2 : (g + 1) * T // 2])
+        halves = (slice(0, T // 2), slice(T // 2, T))
+        for cols in halves:
+            nc.sync.dma_start(gate_sb[0][:, cols], gate[0][:, cols])
+        nc.sync.dma_start(gate_sb[1][:], gate[1])
 
         grouped = {
             e0: keep.tile([P, (e1 - e0) * 4 * C], BF16, name="grouped%d" % e0, align_bytes=ALIGN) for e0, e1 in GROUPS
@@ -294,18 +296,17 @@ def tile_moe_elr_gelu_kernel(
 
         picked = keep.tile([P, T], F32, name="picked")
         prod = [keep.tile([P, T], F32, name="prod%d" % r) for r in range(2)]
-        halves = (slice(0, T // 2), slice(T // 2, T))
         pieces = (halves[0], slice(T // 2, 3 * T // 4), slice(3 * T // 4, T))
         res = [keep.tile([P, c.stop - c.start], F32, name="res%d" % a) for a, c in enumerate(pieces)]
 
         def listed(r, cols):
             return y_sb[:].indirect(pos_sb[r][:, cols.start // 16 : cols.stop // 16])
 
-        for g, cols in enumerate(halves):
+        for cols in halves:
             nc.scalar.activation(picked[:, cols], listed(1, cols), COPY)
-            nc.vector.tensor_tensor(prod[0][:, cols], listed(0, cols), gate_sb[g][:, 0, :], MULT)
-        for g, cols in enumerate(halves):
-            nc.vector.tensor_tensor(prod[1][:, cols], picked[:, cols], gate_sb[g][:, 1, :], MULT)
+            nc.vector.tensor_tensor(prod[0][:, cols], listed(0, cols), gate_sb[0][:, cols], MULT)
+        for cols in halves:
+            nc.vector.tensor_tensor(prod[1][:, cols], picked[:, cols], gate_sb[1][:, cols], MULT)
         for a, cols in enumerate(pieces):
             nc.vector.tensor_tensor(res[a][:], prod[0][:, cols], prod[1][:, cols], ADD)
             nc.sync.dma_start(out[:, cols], res[a][:])

@@ -30,7 +30,7 @@ EARLY = 4
 LATE_ROW = 12
 WB_ROW = 8
 W_GROUP = 4
-SCALAR_REGROUPS = 2
+SCALAR_REGROUPS = 4
 LAG = 2
 HALF_H = H // 2
 GROUPS = ((0, 2), (2, 4), (4, 5), (5, 7), (7, 8))
@@ -136,12 +136,9 @@ def tile_moe_elr_gelu_kernel(
             load_wa(PASSES * e, PASSES * (e + 1))
         load_planes(nc.sync, ws_sb, 0, w_scales, range(2, 4))
 
-        gather_bytes(0, 2 * C)
-        gather_words(0, C)
-        gather_words(C, 2 * C)
-        for e in range(2, E, 2):
-            gather_bytes(e * C, (e + 2) * C)
-            gather_words(e * C, (e + 2) * C)
+        for e0, e1 in ((0, 2), (2, 5), (5, 8)):
+            gather_bytes(e0 * C, e1 * C)
+            gather_words(e0 * C, e1 * C)
 
         for g, (e0, e1) in enumerate(w_groups):
             nc.sync.dma_start(

from contextlib import ExitStack

import concourse.mybir as mybir

K, T, E, C, H, N = 1024, 512, 8, 128, 512, 128
S = E * C
P = 128
PASSES = K // 512
QUADRANTS = 4
LAST = E - 1

F32 = mybir.dt.float32
BF16 = mybir.dt.bfloat16
I32 = mybir.dt.int32
U32 = mybir.dt.uint32
U16 = mybir.dt.uint16
U8 = mybir.dt.uint8
FP8X4 = mybir.dt.float8_e4m3fn_x4
FP4X4 = mybir.dt.float4_e2m1fn_x4
GELU = mybir.ActivationFunctionType.Gelu_apprx_tanh
COPY = mybir.ActivationFunctionType.Copy
MULT = mybir.AluOpType.mult
ADD = mybir.AluOpType.add

FLOPS = 2 * S * (K * H + K * N + H * N)

ALIGN = 256
X_ROW = (0, 4)
EARLY = 4
LATE_ROW = 12
WB_ROW = 8
W_GROUP = 4
SCALAR_REGROUPS = 4
LAG = 2
HALF_H = H // 2
GROUPS = ((0, 2), (2, 4), (4, 5), (5, 7), (7, 8))


def tile_moe_elr_gelu_kernel(
    tc, x_words, x_scales, w_words, w_scales, wa_words, wa_scales, wb_words, wb_scales, gate, offs, pos1, pos2, out
):
    nc = tc.nc
    w_groups = [(e, min(e + W_GROUP, E)) for e in range(0, E, W_GROUP)]
    with ExitStack() as ctx:
        keep = ctx.enter_context(tc.tile_pool(name="keep", bufs=1))
        late = ctx.enter_context(tc.tile_pool(name="late", bufs=1))
        ring = ctx.enter_context(tc.tile_pool(name="ring", bufs=LAG + 2))
        psum_h = ctx.enter_context(tc.psum_pool(name="psum_h", bufs=LAG + 1))
        psum = ctx.enter_context(tc.psum_pool(name="psum", bufs=1))

        offs_sb = keep.tile([P, S // 16], U16, name="offs_sb")
        pos_sb = [keep.tile([P, T // 16], U16, name="pos%d_sb" % r) for r in range(2)]
        x_tok = keep.tile([P, PASSES, T], I32, name="x_tok", align_bytes=ALIGN)
        xs_tok = keep.tile([P, T], U8, name="xs_tok", align_bytes=ALIGN)
        x_slot = [keep.tile([P, S], I32, name="x_slot%d" % s, align_bytes=ALIGN) for s in range(PASSES)]
        xs_slot = [keep.tile([P, S], U8, name="xs_slot%d" % s, align_bytes=ALIGN) for s in range(PASSES)]
        wa_sb = {}
        was_sb = keep.tile([P, EARLY // 2, H], U8, name="was_sb", align_bytes=ALIGN)
        w_sb = [
            keep.tile([P, (e1 - e0) * PASSES, 2 * N], U8, name="w_sb%d" % e0, align_bytes=ALIGN) for e0, e1 in w_groups
        ]
        wb_sb = keep.tile([P, E, N], I32, name="wb_sb", align_bytes=ALIGN)
        gate_sb = [keep.tile([P, T], F32, name="gate_sb%d" % r) for r in range(2)]
        ident = keep.tile([P, P], F32, name="ident")
        y_sb = keep.tile([P, S], F32, name="y_sb")

        def load_wa(first, last, cols=slice(0, H)):
            width = cols.stop - cols.start
            group = keep.tile([P, last - first, width], I32, name="wa_sb%d_%d" % (first, cols.start), align_bytes=ALIGN)
            nc.sync.dma_start(
                group[:], wa_words.rearrange("e s p i d -> p (e s) (i d)").bitcast(I32)[:, first:last, cols]
            )
            for m in range(first, last):
                for a in range(cols.start // HALF_H, cols.stop // HALF_H):
                    wa_sb[m, a] = group[:, m - first, a * HALF_H - cols.start : (a + 1) * HALF_H - cols.start]

        def load_wa_scales(first, last):
            for piece in range(first, last):
                g, q = divmod(piece, QUADRANTS)
                nc.sync.dma_start(
                    was_sb[32 * q : 32 * q + 16, g, :].bitcast(I32),
                    wa_scales[2 * g : 2 * g + 2, :, 4 * q : 4 * q + 4, :]
                    .rearrange("e s r i -> (e s) r i")
                    .bitcast(I32),
                )

        def load_planes(queue, planes, first_row, scales, rows):
            for r in rows:
                queue.dma_start(
                    planes[first_row + r : P : 32, :, :].bitcast(I32),
                    scales.rearrange("e s (q r) n -> r q (e s) n", r=4)[r].bitcast(I32),
                )

        def gather_words(j0, j1):
            for s in range(PASSES):
                nc.vector.tensor_copy(
                    x_slot[s][:, j0:j1].bitcast(U32),
                    x_tok[:, s, :].bitcast(U32).indirect(offs_sb[:, j0 // 16 : j1 // 16]),
                )

        def gather_bytes(j0, j1):
            nc.vector.tensor_copy(xs_slot[0][:, j0:j1], xs_tok[:].indirect(offs_sb[:, j0 // 16 : j1 // 16]))

        nc.vector.memset(xs_tok[:].bitcast(I32), 0)

        late_bytes = (E - EARLY) * PASSES * H
        zeros = late.tile([P, P], F32, name="zeros", align_bytes=ALIGN, offset=late_bytes - ALIGN)
        nc.gpsimd.memset(zeros[:], 0.0)
        nc.gpsimd.affine_select(
            out=ident[:],
            in_=zeros[:],
            compare_op=mybir.AluOpType.not_equal,
            fill=1.0,
            base=0,
            pattern=[[-1, P]],
            channel_multiplier=1,
        )
        was_late = late.tile([P, (E - EARLY) * PASSES, H], U8, name="was_late", align_bytes=ALIGN, offset=0)
        ws_sb = late.tile([P, E * PASSES, N], U8, name="ws_sb", align_bytes=ALIGN, offset=late_bytes)
        load_planes(nc.gpsimd, was_late, LATE_ROW, wa_scales[EARLY:E], range(3))
        load_planes(nc.gpsimd, ws_sb, 0, w_scales, range(2))

        nc.sync.dma_start(x_tok[:], x_words.rearrange("s p t d -> p s (t d)").bitcast(I32))
        for q in range(QUADRANTS):
            nc.sync.dma_start(
                xs_tok[32 * q : 32 * q + 8, :].bitcast(I32), x_scales[:, 4 * q : 4 * q + 4, :].bitcast(I32)
            )
        nc.sync.dma_start(offs_sb[:], offs)
        load_wa(0, 3)
        load_wa_scales(0, QUADRANTS)
        load_wa(3, 6)
        load_wa_scales(QUADRANTS, 2 * QUADRANTS)
        load_wa(6, 8)
        load_planes(nc.sync, was_late, LATE_ROW, wa_scales[EARLY:E], range(3, 4))
        for e in range(EARLY, E):
            load_wa(PASSES * e, PASSES * (e + 1))
        load_planes(nc.sync, ws_sb, 0, w_scales, range(2, 4))

        for e0, e1 in ((0, 2), (2, 5), (5, 8)):
            gather_bytes(e0 * C, e1 * C)
            gather_words(e0 * C, e1 * C)

        for g, (e0, e1) in enumerate(w_groups):
            nc.sync.dma_start(
                w_sb[g][:].bitcast(I32),
                w_words.rearrange("e s p b -> p (e s) b").bitcast(I32)[:, PASSES * e0 : PASSES * e1, :],
            )
            if g == 1:
                for r in range(4):
                    nc.sync.dma_start(
                        xs_slot[1][r:P:32, :].bitcast(I32), xs_slot[0][X_ROW[1] + r : P : 32, :].bitcast(I32)
                    )
        for half in (slice(0, E // 2), slice(E // 2, E)):
            nc.sync.dma_start(
                wb_sb[:, half, :], wb_words.rearrange("e o p n d -> p (e o) (n d)").bitcast(I32)[:, half, :]
            )
        nc.sync.dma_start(pos_sb[1][:], pos2)
        nc.sync.dma_start(pos_sb[0][:], pos1)
        halves = (slice(0, T // 2), slice(T // 2, T))
        for cols in halves:
            nc.sync.dma_start(gate_sb[0][:, cols], gate[0][:, cols])
        nc.sync.dma_start(gate_sb[1][:], gate[1])

        grouped = {
            e0: keep.tile([P, (e1 - e0) * 4 * C], BF16, name="grouped%d" % e0, align_bytes=ALIGN) for e0, e1 in GROUPS
        }
        group_of = {e: e0 for e0, e1 in GROUPS for e in range(e0, e1)}
        h_codes = keep.tile([P, S], U32, name="h_codes", align_bytes=ALIGN)
        h_scales = keep.tile([P, S], U8, name="h_scales", align_bytes=ALIGN)
        banks = {}
        h_rows = {}
        turned = {}

        def first_product(e):
            cols = slice(e * C, (e + 1) * C)
            banks[e] = [psum_h.tile([P, H], F32, name="bank%d" % a) for a in range(2)]
            for a in range(2):
                hid = slice(a * HALF_H, (a + 1) * HALF_H)
                for s in range(PASSES):
                    nc.tensor.matmul_mx(
                        banks[e][a][:, 0:HALF_H],
                        lhsT=x_slot[s][:, cols].bitcast(FP8X4),
                        lhsT_scale=xs_slot[0][X_ROW[s] : P, cols],
                        rhs=wa_sb[PASSES * e + s, a].bitcast(FP8X4),
                        rhs_scale=(
                            was_sb[4 * (PASSES * (e % 2) + s) : P, e // 2, hid]
                            if e < EARLY
                            else was_late[LATE_ROW:P, PASSES * (e - EARLY) + s, hid]
                        ),
                        start=(s == 0),
                        stop=(s == PASSES - 1),
                    )

        def activate(e, a):
            if a == 0:
                h_rows[e] = ring.tile([P, H], BF16, name="h", align_bytes=ALIGN)
            nc.scalar.activation(
                h_rows[e][:].rearrange("j (u p b) -> j u p b", u=2, b=2)[:, :, P // 2 * a : P // 2 * (a + 1), :],
                banks[e][a][:, 0:HALF_H].rearrange("j (p u b) -> j u p b", u=2, b=2),
                GELU,
            )

        def turn(e, bank, first=HALF_H):
            words = h_rows[e][:].bitcast(F32)
            turned[e] = bank[:, first : first + HALF_H].rearrange("p (u j) -> p u j", u=2)
            for u in range(2):
                nc.tensor.transpose(turned[e][:, u, :], words[:, u * P : (u + 1) * P], ident[:])

        def regroup(e, copy):
            copy(
                grouped[group_of[e]][:].bitcast(F32).rearrange("p (e j u) -> p e j u", j=C, u=2)[:, e - group_of[e]],
                turned[e].rearrange("p u j -> p j u"),
            )

        def quantise(e0, e1):
            cols = slice(e0 * C, e1 * C)
            nc.vector.quantize_mx(
                h_codes[:, cols].bitcast(FP8X4),
                h_scales[:, cols],
                grouped[e0][:],
            )

        def adapter_pass(acc, e, opens):
            cols = slice(e * C, (e + 1) * C)
            nc.tensor.matmul_mx(
                acc,
                lhsT=wb_sb[:, e, :].bitcast(FP8X4),
                lhsT_scale=wbs_sb[WB_ROW:P, e, :],
                rhs=h_codes[:, cols].bitcast(FP8X4),
                rhs_scale=h_scales[:, cols],
                start=opens,
                stop=not opens,
            )

        def frozen_pass(acc, e, s):
            cols = slice(e * C, (e + 1) * C)
            nc.tensor.matmul_mx(
                acc,
                lhsT=w_sb[e // W_GROUP][:, PASSES * (e % W_GROUP) + s, :].bitcast(FP4X4),
                lhsT_scale=ws_sb[:, PASSES * e + s, :],
                rhs=x_slot[s][:, cols].bitcast(FP8X4),
                rhs_scale=xs_slot[s][:, cols],
                start=(s == 0),
                stop=False,
            )

        for e in range(LAST):
            first_product(e)
            if e == 1:
                wbs_sb = keep.tile([P, E, N], U8, name="wa_sb0_0", align_bytes=ALIGN)
                load_planes(nc.gpsimd, wbs_sb, WB_ROW, wb_scales, range(4))
            if e in (2, 4):
                activate(e, 0)
                turn(e - 2, banks[e][1])
                turn(e - 1, banks[e][0])
                activate(e, 1)
                for d in (e - 2, e - 1):
                    regroup(d, nc.scalar.copy if d < SCALAR_REGROUPS else nc.vector.tensor_copy)
                quantise(e - 2, e)
            elif e == 5:
                activate(e, 0)
                turn(e - 1, banks[e][1])
                activate(e, 1)
                regroup(e - 1, nc.vector.tensor_copy)
                quantise(e - 1, e)
            else:
                activate(e, 0)
                activate(e, 1)

        first_product(LAST)
        activate(LAST, 0)
        turn(LAST - 2, banks[LAST][0], 0)
        turn(LAST - 1, banks[LAST][0])
        activate(LAST, 1)
        nc.vector.tensor_copy(
            grouped[LAST - 2][:].bitcast(F32).rearrange("p (e j u) -> p e j u", j=C, u=2),
            banks[LAST][0][:].rearrange("p (e u j) -> p e j u", e=2, u=2),
        )
        quantise(LAST - 2, LAST)
        turn(LAST, banks[LAST][1])
        regroup(LAST, nc.scalar.copy)
        quantise(LAST, E)

        sums = [psum.tile([P, H], F32, name="spare%d" % k) for k in range(2)]
        sums.extend(psum_h.tile([P, H], F32, name="bank%d" % (k % 2)) for k in range(E - 2))
        for s in range(PASSES):
            for e in range(E):
                frozen_pass(sums[e][:, 0:C], e, s)
        for e in range(E):
            adapter_pass(sums[e][:, 0:C], e, False)
            evacuate = nc.scalar.copy if e % 2 else nc.vector.tensor_copy
            evacuate(y_sb[:, e * C : (e + 1) * C], sums[e][:, 0:C])

        picked = keep.tile([P, T], F32, name="picked")
        prod = [keep.tile([P, T], F32, name="prod%d" % r) for r in range(2)]
        pieces = (halves[0], slice(T // 2, 3 * T // 4), slice(3 * T // 4, T))
        res = [keep.tile([P, c.stop - c.start], F32, name="res%d" % a) for a, c in enumerate(pieces)]

        def listed(r, cols):
            return y_sb[:].indirect(pos_sb[r][:, cols.start // 16 : cols.stop // 16])

        for cols in halves:
            nc.scalar.activation(picked[:, cols], listed(1, cols), COPY)
            nc.vector.tensor_tensor(prod[0][:, cols], listed(0, cols), gate_sb[0][:, cols], MULT)
        for cols in halves:
            nc.vector.tensor_tensor(prod[1][:, cols], picked[:, cols], gate_sb[1][:, cols], MULT)
        for a, cols in enumerate(pieces):
            nc.vector.tensor_tensor(res[a][:], prod[0][:, cols], prod[1][:, cols], ADD)
            nc.sync.dma_start(out[:, cols], res[a][:])
